import numpy as np
import ml_dtypes


def mxq(x, axis, fmt="e4m3"):
    dtype, down = {"e4m3": (ml_dtypes.float8_e4m3fn, 7), "e5m2": (ml_dtypes.float8_e5m2, 14)}[fmt]
    v = np.moveaxis(np.asarray(x, np.float32).astype(ml_dtypes.bfloat16).astype(np.float64), axis, -1)
    blocks = v.reshape(v.shape[:-1] + (-1, 32))
    amax = np.abs(blocks).max(-1, keepdims=True)
    byte = np.maximum(np.where(amax > 0, np.frexp(amax)[1] - 1 + 127, 0) - down, 1)
    scale = np.exp2(byte - 127.0)
    codes = (blocks / scale).astype(np.float32).astype(dtype).astype(np.float64)
    return np.moveaxis((codes * scale).reshape(v.shape), -1, axis)


WIDE = False


def mx_kscale(k):
    if not WIDE:
        return np.ones(k)
    levels = np.array([10, -10, 5, -5, 0])
    if k % 512:
        return np.exp2(np.random.permutation(np.resize(levels, k // 32))).repeat(32)
    a = np.empty((k // 512, 16))
    for p in range(k // 512):
        a[p, :8] = np.random.permutation(np.resize(levels, 8))
        for g in range(8):
            far = levels[np.abs(levels - a[p, g]) >= 10]
            a[p, g + 8] = far[np.random.randint(len(far))]
    return np.exp2(a.ravel()).repeat(32)


def f64(x):
    return np.asarray(x).astype(np.float64)


def striped(idx):
    return np.tile(idx.reshape(-1, 16).T, (8, 1)).astype(np.uint16)


def unstriped(offs):
    return offs[:16].T.reshape(-1).astype(np.int64)


E2M1 = np.array([0.0, 0.5, 1.0, 1.5, 2.0, 3.0, 4.0, 6.0, -0.0, -0.5, -1.0, -1.5, -2.0, -3.0, -4.0, -6.0])


def pack_weight(w, fmt):
    k, n = w.shape
    w = f64(np.asarray(w, np.float32).astype(ml_dtypes.bfloat16)).reshape(k // 32, 32, n)
    amax = np.abs(w).max(1)
    if fmt == "e4m3":
        byte = np.frexp(amax)[1] - 1 + 127 - 7
    else:
        mant, ex = np.frexp(amax / 6.0)
        byte = np.where(mant > 0.5, ex, ex - 1) + 127
    byte = np.clip(np.where(amax > 0, byte, 1), 1, 254)
    scaled = (w * np.exp2(127.0 - byte)[:, None, :]).reshape(k, n).astype(np.float32)
    by_word = np.ascontiguousarray(scaled.reshape(k // 512, 128, 4, n).transpose(0, 1, 3, 2))
    if fmt == "e4m3":
        words = by_word.astype(ml_dtypes.float8_e4m3fn).view(np.uint8)
    else:
        c = by_word.astype(ml_dtypes.float4_e2m1fn).view(np.uint8) & 0xF
        words = (c[..., 0::2] | (c[..., 1::2] << 4)).reshape(k // 512, 128, 2 * n)
    return np.ascontiguousarray(words), np.ascontiguousarray(byte.astype(np.uint8).reshape(k // 512, 16, n))


def unpack_weight(words, scales, fmt):
    g, _, n = scales.shape
    words = np.ascontiguousarray(words).reshape(g, 128, n, -1)
    if fmt == "e4m3":
        vals = words.view(ml_dtypes.float8_e4m3fn).astype(np.float64)
    else:
        nib = np.empty((g, 128, n, 4), np.uint8)
        nib[..., 0::2] = words & 0xF
        nib[..., 1::2] = words >> 4
        vals = E2M1[nib]
    vals = vals * np.repeat(np.exp2(scales.astype(np.float64) - 127.0), 8, axis=1)[..., None]
    return vals.transpose(0, 1, 3, 2).reshape(g * 512, n)


def gelu(v):
    return 0.5 * v * (1.0 + np.tanh(np.sqrt(2.0 / np.pi) * (v + 0.044715 * v**3)))


T, S, K, KA, KB, H, T3, S2, P = 4096, 1024, 1536, 512, 1024, 1024, 2048, 512, 512

def setup_inputs():
    n = np.random.standard_normal
    s = mx_kscale(K)[:, None]
    u = mx_kscale(H)[:, None]
    tab_words, tab_scales = pack_weight(n((K, T)) * s, "e4m3")
    tab2_words, tab2_scales = pack_weight(n((H, T3)) / np.sqrt(H) / u, "e4m3")
    w4_words, w4_scales = pack_weight(n((KB, H)) / np.sqrt(K) / s[KA:], "e2m1")
    sign = np.where(np.random.uniform(0, 1, S2) < 0.5, -1.0, 1.0)
    return {
        "tab_words": tab_words, "tab_scales": tab_scales,
        "offs": striped(np.random.permutation(T)[:S]),
        "w1": (n((KA, H)) / np.sqrt(K) / s[:KA]).astype(np.float32),
        "w4_words": w4_words, "w4_scales": w4_scales,
        "b1": (0.6 * n(H)).astype(np.float32),
        "gain": (np.random.uniform(0.8, 1.7, H) * u[:, 0]).astype(np.float32),
        "tab2_words": tab2_words, "tab2_scales": tab2_scales,
        "offs2": striped(np.random.permutation(T3)[:S2]),
        "pos1": striped(np.random.permutation(S)[:P]),
        "pos2": striped(np.random.permutation(S)[:P]),
        "temp": np.random.uniform(0.4, 1.6, S2).astype(np.float32),
        "load": (sign * np.random.uniform(3.0, 6.0, S2)).astype(np.float32),
        "finish": np.random.uniform(0.4, 1.2, S2).astype(np.float32),
    }

def reference(tab_words, tab_scales, offs, w1, w4_words, w4_scales, b1, gain,
              tab2_words, tab2_scales, offs2, pos1, pos2, temp, load, finish):
    v = unpack_weight(tab_words, tab_scales, "e4m3")[:, unstriped(offs)]
    v2 = unpack_weight(tab2_words, tab2_scales, "e4m3")[:, unstriped(offs2)]
    w1q = mxq(f64(w1), 0, "e4m3")
    w4 = unpack_weight(w4_words, w4_scales, "e2m1")
    f = w1q.T @ v[:KA] + w4.T @ v[KA:]
    h = f64(gain)[:, None] * np.tanh(f + f64(b1)[:, None])
    e = v2.T @ mxq(h, 0, "e4m3")
    top = e.max(axis=1)
    a = np.exp(f64(temp)[:, None] * (e[:, unstriped(pos1)] - top[:, None]))
    c = e[:, unstriped(pos2)]
    return f64(load)[:, None] * a + f64(finish)[:, None] * c

@@ -1,0 +1,283 @@
+from contextlib import ExitStack
+
+import concourse.mybir as mybir
+
+T, S, K, KA, KB, H, T3, S2, NP = 4096, 1024, 1536, 512, 1024, 1024, 2048, 512, 512
+FLOPS = 2 * K * H * S + 2 * H * S2 * S
+
+F32 = mybir.dt.float32
+BF16 = mybir.dt.bfloat16
+I32 = mybir.dt.int32
+U32 = mybir.dt.uint32
+U16 = mybir.dt.uint16
+U8 = mybir.dt.uint8
+FP8X4 = mybir.dt.float8_e4m3fn_x4
+FP4X4 = mybir.dt.float4_e2m1fn_x4
+ALU = mybir.AluOpType
+ACT = mybir.ActivationFunctionType
+
+P = 128
+PACK = 4
+NB = 512
+SHIFT_ROWS = 112
+
+
+def tile_list_fastener_job_looks_kernel(tc, tab_words, tab_scales, offs, w1, w4_words, w4_scales, b1, gain,
+                                                  tab2_words, tab2_scales, offs2, pos1, pos2, temp, load, finish, out):
+    nc = tc.nc
+    SQ = nc.gpsimd
+    MQ = nc.gpsimd
+    with ExitStack() as ctx:
+        lists = ctx.enter_context(tc.tile_pool(name="lists", bufs=1))
+        keep = ctx.enter_context(tc.tile_pool(name="keep", bufs=1))
+        ring = ctx.enter_context(tc.tile_pool(name="ring", bufs=2))
+        psum = ctx.enter_context(tc.psum_pool(name="psum", bufs=1))
+
+        def held(shape, dtype, name):
+            return keep.tile(shape, dtype, name=name, align_bytes=64)
+
+        offs_t = lists.tile([P, S // 16], U16, name="offs_t")
+        offs2_t = lists.tile([P, S2 // 16], U16, name="offs2_t")
+        pos1_t = lists.tile([P, NP // 16], U16, name="pos1_t")
+        pos2_t = lists.tile([P, NP // 16], U16, name="pos2_t")
+
+        tab_s = held([P, T], U8, "tab_s")
+        w4_s_raw = held([P, 2, H], U8, "w4_s_raw")
+        tab2_s = held([P, T3], U8, "tab2_s")
+        v_s_shift = [held([P, S], U8, "v_s_shift%d" % a) for a in (1, 2)]
+        nc.vector.memset(tab_s[:].bitcast(I32), 0)
+        nc.vector.memset(w4_s_raw[:].rearrange("p a c -> p (a c)").bitcast(I32), 0)
+        nc.vector.memset(tab2_s[:].bitcast(I32), 0)
+        for t in v_s_shift:
+            nc.vector.memset(t[:].bitcast(I32), 0)
+
+        w4_raw = held([P, 2, 2 * H], U8, "w4_raw")
+        w1_raw = [held([P, PACK, NB], F32, "w1_raw%d" % b) for b in range(2)]
+        tab_w = [held([P, T], U32, "tab_w%d" % a) for a in range(3)]
+        tab2_w = [held([P, T3], U32, "tab2_w%d" % a) for a in range(2)]
+        b1_t = held([P, 2, PACK], F32, "b1_t")
+        gain_t = held([P, 2, PACK], F32, "gain_t")
+        temp_t = held([P, 4], F32, "temp_t")
+        load_t = held([P, 4], F32, "load_t")
+        finish_t = held([P, 4], F32, "finish_t")
+
+        def load_w1(b):
+            nc.sync.dma_start(out=w1_raw[b][:], in_=w1[:, NB * b:NB * (b + 1)].rearrange("(p j) c -> p j c", j=PACK))
+
+        def load_words(dst, src):
+            nc.sync.dma_start(out=dst[:].bitcast(I32), in_=src.rearrange("p t i -> p (t i)").bitcast(I32))
+
+        nc.scalar.dma_start(out=b1_t[:], in_=b1.rearrange("(b p i) -> p b i", b=2, i=PACK))
+        nc.scalar.dma_start(out=gain_t[:], in_=gain.rearrange("(b p i) -> p b i", b=2, i=PACK))
+        nc.sync.dma_start(offs_t[:], offs)
+        nc.sync.dma_start(offs2_t[:], offs2)
+        nc.sync.dma_start(out=w4_raw[:].bitcast(I32), in_=w4_words.rearrange("a p n -> p a n").bitcast(I32))
+        load_w1(0)
+        for q in range(4):
+            SQ.dma_start(out=tab_s[32 * q:32 * q + 12, :].bitcast(I32),
+                                in_=tab_scales[:, 4 * q:4 * q + 4, :].bitcast(I32))
+        load_words(tab_w[0], tab_words[0])
+        for q in range(4):
+            SQ.dma_start(out=w4_s_raw[32 * q:32 * q + 4, :, :].bitcast(I32),
+                                in_=w4_scales[:, 4 * q:4 * q + 4, :].rearrange("a r c -> r a c").bitcast(I32))
+        load_words(tab_w[1], tab_words[1])
+        for q in range(4):
+            SQ.dma_start(out=tab2_s[32 * q:32 * q + 8, :].bitcast(I32),
+                                in_=tab2_scales[:, 4 * q:4 * q + 4, :].bitcast(I32))
+        load_words(tab_w[2], tab_words[2])
+        load_w1(1)
+        for a in range(2):
+            load_words(tab2_w[a], tab2_words[a])
+        nc.sync.dma_start(pos1_t[:], pos1)
+        nc.sync.dma_start(pos2_t[:], pos2)
+        with nc.allow_non_contiguous_dma(reason="one value a job, jobs on the partitions"):
+            for dst, src in ((temp_t, temp), (load_t, load), (finish_t, finish)):
+                nc.sync.dma_start(out=dst[:], in_=src.rearrange("(m p) -> p m", p=P))
+
+        w4_c = held([P, 2, 2 * H], U8, "w4_c")
+        nc.vector.tensor_copy(
+            out=w4_c[:].bitcast(U16).rearrange("p a (b t m) -> p (a b) t m", b=2, t=PACK),
+            in_=w4_raw[:].bitcast(U16).rearrange("p a (b m t) -> p (a b) t m", b=2, t=PACK))
+
+        v_s = held([P, S], U8, "v_s")
+        nc.vector.tensor_copy(out=v_s[:], in_=tab_s[:].indirect(offs_t[:]))
+        for a in (1, 2):
+            MQ.dma_start(out=v_s_shift[a - 1][0:SHIFT_ROWS, :].bitcast(I32),
+                                in_=v_s[4 * a:4 * a + SHIFT_ROWS, :].bitcast(I32))
+        v_planes = [v_s, v_s_shift[0], v_s_shift[1]]
+
+        w4_s = held([P, 2, H], U8, "w4_s")
+        nc.vector.tensor_copy(
+            out=w4_s[:].rearrange("p a (b t m) -> p (a b) t m", b=2, t=PACK),
+            in_=w4_s_raw[:].rearrange("p a (b m t) -> p (a b) t m", b=2, t=PACK))
+
+        v2_s = held([P, S2], U8, "v2_s")
+        nc.vector.tensor_copy(out=v2_s[:], in_=tab2_s[:].indirect(offs2_t[:]))
+
+        def grouped(h):
+            return keep.tile([P, NB * PACK], BF16, name="grouped%d" % h, tag="grouped%d" % h, align_bytes=64)
+
+        w1_g = [grouped(1), grouped(0)]
+        w1_c = [held([P, NB], U32, "w1_c%d" % b) for b in range(2)]
+        w1_s = [held([P, NB], U8, "w1_s%d" % b) for b in range(2)]
+
+        def round_w1(b, copy):
+            copy(out=w1_g[b][:].rearrange("p (t m j) -> p m t j", t=PACK, j=PACK),
+                 in_=w1_raw[b][:].rearrange("p j (m t) -> p m t j", t=PACK))
+
+        def quantise_w1(b):
+            nc.vector.quantize_mx(out=w1_c[b][:].bitcast(FP8X4), scales=w1_s[b][:], in_=w1_g[b][:])
+
+        round_w1(0, nc.scalar.copy)
+        quantise_w1(0)
+
+        v_w = [[held([P, NB], U32, "v_w%d_%d" % (a, h)) for h in range(2)] for a in range(3)]
+
+        def gather_words(a):
+            for h in range(2):
+                nc.vector.tensor_copy(out=v_w[a][h][:], in_=tab_w[a][:].indirect(offs_t[:, 32 * h:32 * (h + 1)]))
+
+        def bank(h, i):
+            return psum.tile([P, NB], F32, name="bank%d_%d" % (h, i), tag="bank%d_%d" % (h, i))
+
+        def first_pass(acc, a, b, h, i, order):
+            cols = slice(NB * h, NB * (h + 1))
+            if a == 0:
+                lhsT = w1_c[b][:, P * i:P * (i + 1)].bitcast(FP8X4)
+                lhsT_scale = w1_s[b][:, P * i:P * (i + 1)]
+            else:
+                c0 = NB * b + P * i
+                lhsT = w4_c[:, a - 1, 2 * c0:2 * (c0 + P)].bitcast(FP4X4)
+                lhsT_scale = w4_s[:, a - 1, c0:c0 + P]
+            nc.tensor.matmul_mx(out=acc[:], lhsT=lhsT, lhsT_scale=lhsT_scale, rhs=v_w[a][h][:].bitcast(FP8X4),
+                                rhs_scale=v_planes[a][:, cols], start=(a == order[0]), stop=(a == order[2]))
+
+        def tanh_of(acc, b):
+            th = ring.tile([P, PACK, NB], F32, name="th", tag="th", bufs=3)
+            for i in range(PACK):
+                nc.scalar.activation(out=th[:, i, :], in_=acc[i][:], func=ACT.Tanh, bias=b1_t[:, b, i:i + 1])
+            return th
+
+        h_c = [[held([P, NB], U32, "h_c%d_%d" % (b, h)) for h in range(2)] for b in range(2)]
+        h_s = [[held([P, NB], U8, "h_s%d_%d" % (b, h)) for h in range(2)] for b in range(2)]
+
+        def apply_gain(th, b, h):
+            hb = grouped(h)
+            nc.vector.tensor_tensor(
+                out=hb[:].rearrange("p (c u t) -> p c t u", u=2, t=PACK),
+                in0=th[:].rearrange("p t (c u) -> p c t u", u=2),
+                in1=gain_t[:, b, :].unsqueeze(1).unsqueeze(3).to_broadcast([P, NB // 2, PACK, 2]),
+                op=ALU.mult)
+            return hb
+
+        def apply_gain_scalar(th, b):
+            hp = held([P, PACK, NB], BF16, "hp")
+            for i in range(PACK):
+                nc.scalar.activation(out=hp[:, i, :], in_=th[:, i, :], func=ACT.Copy, scale=gain_t[:, b, i:i + 1])
+            hb = held([P, NB * PACK], BF16, "hb_last")
+            nc.scalar.copy(out=hb[:].rearrange("p (c u t) -> p c t u", u=2, t=PACK),
+                           in_=hp[:].rearrange("p t (c u) -> p c t u", u=2))
+            return hb
+
+        def quantise_h(hb, b, h):
+            nc.vector.quantize_mx(out=h_c[b][h][:].bitcast(FP8X4), scales=h_s[b][h][:], in_=hb[:])
+
+        acc = {}
+        for h in range(2):
+            acc[0, h] = [bank(h, i) for i in range(PACK)]
+        for a in range(3):
+            gather_words(a)
+            for h in range(2):
+                for i in range(PACK):
+                    first_pass(acc[0, h][i], a, 0, h, i, (0, 1, 2))
+
+        round_w1(1, nc.vector.tensor_copy)
+        th00 = tanh_of(acc[0, 0], 0)
+        quantise_w1(1)
+        th01 = tanh_of(acc[0, 1], 0)
+        for h in range(2):
+            acc[1, h] = [bank(h, i) for i in range(PACK)]
+            for i in range(PACK):
+                for a in (1, 2, 0):
+                    first_pass(acc[1, h][i], a, 1, h, i, (1, 2, 0))
+        hb00 = apply_gain(th00, 0, 0)
+        th10 = tanh_of(acc[1, 0], 1)
+        hb01 = apply_gain(th01, 0, 1)
+        quantise_h(hb00, 0, 0)
+        th11 = tanh_of(acc[1, 1], 1)
+
+        v2_w = [held([P, S2], U32, "v2_w%d" % a) for a in range(2)]
+
+        def gather_jobs(a):
+            nc.vector.tensor_copy(out=v2_w[a][:], in_=tab2_w[a][:].indirect(offs2_t[:]))
+
+        gather_jobs(0)
+        quantise_h(hb01, 0, 1)
+        hb10 = apply_gain(th10, 1, 0)
+        gather_jobs(1)
+        quantise_h(hb10, 1, 0)
+        hb11 = apply_gain_scalar(th11, 1)
+
+        def second_pass(dst, a, h, m):
+            cols = slice(P * m, P * (m + 1))
+            nc.tensor.matmul_mx(out=dst[:], lhsT=v2_w[a][:, cols].bitcast(FP8X4), lhsT_scale=v2_s[4 * a:P, cols],
+                                rhs=h_c[a][h][:].bitcast(FP8X4), rhs_scale=h_s[a][h][:], start=(a == 0), stop=(a == 1))
+
+        neg_temp = held([P, 4], F32, "neg_temp")
+        nc.vector.tensor_scalar(out=neg_temp[:], in0=temp_t[:], scalar1=-1.0, scalar2=None, op0=ALU.mult)
+        e = [held([P, S], F32, "e%d" % m) for m in range(4)]
+        top_half = held([P, 4], F32, "top_half")
+        top = held([P, 4], F32, "top")
+        look_bias = held([P, 4], F32, "look_bias")
+
+        sc = {}
+        for h in range(2):
+            sc[h] = [bank(h, m) for m in range(4)]
+        for m in range(4):
+            for a in range(2):
+                second_pass(sc[0][m], a, 0, m)
+        for m in range(4):
+            second_pass(sc[1][m], 0, 1, m)
+
+        def scores_out(h, m):
+            nc.vector.tensor_scalar(out=e[m][:, NB * h:NB * (h + 1)], in0=sc[h][m][:], scalar1=1.0,
+                                    scalar2=(None if h == 0 else top_half[:, m:m + 1]), op0=ALU.mult, op1=ALU.max,
+                                    accum_out=(top_half if h == 0 else top)[:, m:m + 1])
+
+        for m in range(3):
+            scores_out(0, m)
+        quantise_h(hb11, 1, 1)
+        for m in range(4):
+            second_pass(sc[1][m], 1, 1, m)
+        scores_out(0, 3)
+
+        def look(m):
+            nc.scalar.activation(out=look_bias[:, m:m + 1], in_=top[:, m:m + 1], func=ACT.Copy,
+                                 scale=neg_temp[:, m:m + 1])
+            a_t = ring.tile([P, NP], F32, name="a_t", tag="a_t")
+            nc.scalar.activation(out=a_t[:], in_=e[m][:].indirect(pos1_t[:]), func=ACT.Exp,
+                                 bias=look_bias[:, m:m + 1], scale=temp_t[:, m:m + 1])
+            la = ring.tile([P, NP], F32, name="la", tag="la", bufs=4)
+            nc.scalar.activation(out=la[:], in_=a_t[:], func=ACT.Copy, scale=load_t[:, m:m + 1])
+            return la
+
+        def pick(m):
+            c_t = ring.tile([P, NP], F32, name="c_t", tag="c_t", bufs=4)
+            nc.vector.tensor_copy(out=c_t[:], in_=e[m][:].indirect(pos2_t[:]))
+            return c_t
+
+        def finish_rows(m, c_t, la):
+            o_t = ring.tile([P, NP], F32, name="o_t", tag="o_t", bufs=4)
+            nc.vector.scalar_tensor_tensor(out=o_t[:], in0=c_t[:], scalar=finish_t[:, m:m + 1], in1=la[:],
+                                           op0=ALU.mult, op1=ALU.add)
+            nc.sync.dma_start(out=out[P * m:P * (m + 1), :], in_=o_t[:])
+
+        la, c_t = {}, {}
+        for step in range(6):
+            if step < 4:
+                scores_out(1, step)
+                la[step] = look(step)
+            if 1 <= step < 5:
+                c_t[step - 1] = pick(step - 1)
+            if 2 <= step:
+                finish_rows(step - 2, c_t[step - 2], la[step - 2])

@@ -19,100 +19,97 @@ ACT = mybir.ActivationFunctionType
 P = 128
 PACK = 4
 NB = 512
-SHIFT_ROWS = 112
 
 
 def tile_list_fastener_job_looks_kernel(tc, tab_words, tab_scales, offs, w1, w4_words, w4_scales, b1, gain,
                                                   tab2_words, tab2_scales, offs2, pos1, pos2, temp, load, finish, out):
     nc = tc.nc
-    SQ = nc.gpsimd
-    MQ = nc.gpsimd
     with ExitStack() as ctx:
         lists = ctx.enter_context(tc.tile_pool(name="lists", bufs=1))
         keep = ctx.enter_context(tc.tile_pool(name="keep", bufs=1))
+        stage = ctx.enter_context(tc.tile_pool(name="stage", bufs=1))
         ring = ctx.enter_context(tc.tile_pool(name="ring", bufs=2))
         psum = ctx.enter_context(tc.psum_pool(name="psum", bufs=1))
 
-        def held(shape, dtype, name):
-            return keep.tile(shape, dtype, name=name, align_bytes=64)
+        def held(shape, dtype, name, after=None):
+            return keep.tile(shape, dtype, name=name, tag=(after or name), align_bytes=64)
 
+        def staged(shape, dtype, name, offset):
+            return stage.tile(shape, dtype, name=name, align_bytes=64, offset=offset)
+
+        REGION = 4 * T
         offs_t = lists.tile([P, S // 16], U16, name="offs_t")
         offs2_t = lists.tile([P, S2 // 16], U16, name="offs2_t")
         pos1_t = lists.tile([P, NP // 16], U16, name="pos1_t")
         pos2_t = lists.tile([P, NP // 16], U16, name="pos2_t")
 
-        tab_s = held([P, T], U8, "tab_s")
-        w4_s_raw = held([P, 2, H], U8, "w4_s_raw")
-        tab2_s = held([P, T3], U8, "tab2_s")
-        v_s_shift = [held([P, S], U8, "v_s_shift%d" % a) for a in (1, 2)]
+        tab_s = staged([P, T], U8, "tab_s", REGION)
+        w4_s_raw = staged([P, 2, H], U8, "w4_s_raw", 2 * REGION)
+        v_s = held([P, 3, S], U8, "v_s")
+        v2_s = held([P, 2, S2], U8, "v2_s")
         nc.vector.memset(tab_s[:].bitcast(I32), 0)
-        nc.vector.memset(w4_s_raw[:].rearrange("p a c -> p (a c)").bitcast(I32), 0)
-        nc.vector.memset(tab2_s[:].bitcast(I32), 0)
-        for t in v_s_shift:
-            nc.vector.memset(t[:].bitcast(I32), 0)
+        for t in (w4_s_raw, v_s, v2_s):
+            nc.vector.memset(t[:].rearrange("p a c -> p (a c)").bitcast(I32), 0)
 
-        w4_raw = held([P, 2, 2 * H], U8, "w4_raw")
-        w1_raw = [held([P, PACK, NB], F32, "w1_raw%d" % b) for b in range(2)]
-        tab_w = [held([P, T], U32, "tab_w%d" % a) for a in range(3)]
-        tab2_w = [held([P, T3], U32, "tab2_w%d" % a) for a in range(2)]
-        b1_t = held([P, 2, PACK], F32, "b1_t")
-        gain_t = held([P, 2, PACK], F32, "gain_t")
-        temp_t = held([P, 4], F32, "temp_t")
-        load_t = held([P, 4], F32, "load_t")
-        finish_t = held([P, 4], F32, "finish_t")
+        w4_raw = [staged([P, 2 * H], U8, "w4_raw%d" % a, 3 * a * REGION) for a in range(2)]
 
-        def load_w1(b):
-            nc.sync.dma_start(out=w1_raw[b][:], in_=w1[:, NB * b:NB * (b + 1)].rearrange("(p j) c -> p j c", j=PACK))
+        def load_w1(b, raw):
+            nc.sync.dma_start(out=raw[:], in_=w1[:, NB * b:NB * (b + 1)].rearrange("(p j) c -> p j c", j=PACK))
+            return raw
 
-        def load_words(dst, src):
+        def load_words(src, name, offset):
+            dst = staged([P, src.shape[1]], U32, name, offset)
             nc.sync.dma_start(out=dst[:].bitcast(I32), in_=src.rearrange("p t i -> p (t i)").bitcast(I32))
+            return dst
 
-        nc.scalar.dma_start(out=b1_t[:], in_=b1.rearrange("(b p i) -> p b i", b=2, i=PACK))
-        nc.scalar.dma_start(out=gain_t[:], in_=gain.rearrange("(b p i) -> p b i", b=2, i=PACK))
+        def load_scale_rows(dst, row0, src):
+            rows = src.shape[0] * src.shape[1]
+            nc.sync.dma_start(out=dst[row0:row0 + rows, :].bitcast(I32),
+                              in_=src.rearrange("a q c -> q a c").bitcast(I32))
+
+        def spread_scale_rows(planes, picked, row0, first, passes):
+            for q in range(4):
+                nc.sync.dma_start(out=planes[32 * q:32 * q + 4, first:first + passes, :].bitcast(I32),
+                                  in_=picked[row0 + 4 * passes * q:row0 + 4 * passes * (q + 1), :].bitcast(I32))
+
+        nc.sync.dma_start(out=w4_raw[0][:].bitcast(I32), in_=w4_words[0].bitcast(I32))
         nc.sync.dma_start(offs_t[:], offs)
         nc.sync.dma_start(offs2_t[:], offs2)
-        nc.sync.dma_start(out=w4_raw[:].bitcast(I32), in_=w4_words.rearrange("a p n -> p a n").bitcast(I32))
-        load_w1(0)
-        for q in range(4):
-            SQ.dma_start(out=tab_s[32 * q:32 * q + 12, :].bitcast(I32),
-                                in_=tab_scales[:, 4 * q:4 * q + 4, :].bitcast(I32))
-        load_words(tab_w[0], tab_words[0])
-        for q in range(4):
-            SQ.dma_start(out=w4_s_raw[32 * q:32 * q + 4, :, :].bitcast(I32),
-                                in_=w4_scales[:, 4 * q:4 * q + 4, :].rearrange("a r c -> r a c").bitcast(I32))
-        load_words(tab_w[1], tab_words[1])
-        for q in range(4):
-            SQ.dma_start(out=tab2_s[32 * q:32 * q + 8, :].bitcast(I32),
-                                in_=tab2_scales[:, 4 * q:4 * q + 4, :].bitcast(I32))
-        load_words(tab_w[2], tab_words[2])
-        load_w1(1)
-        for a in range(2):
-            load_words(tab2_w[a], tab2_words[a])
         nc.sync.dma_start(pos1_t[:], pos1)
         nc.sync.dma_start(pos2_t[:], pos2)
-        with nc.allow_non_contiguous_dma(reason="one value a job, jobs on the partitions"):
-            for dst, src in ((temp_t, temp), (load_t, load), (finish_t, finish)):
-                nc.sync.dma_start(out=dst[:], in_=src.rearrange("(m p) -> p m", p=P))
+        nc.sync.dma_start(out=w4_raw[1][:].bitcast(I32), in_=w4_words[1].bitcast(I32))
+        w1_raw = [load_w1(0, held([P, PACK, NB], F32, "w1_raw0")), None]
+        load_scale_rows(tab_s, 0, tab_scales[0:2])
+        load_scale_rows(tab_s, 32, tab_scales[2:3])
+        for q in range(4):
+            nc.sync.dma_start(out=w4_s_raw[32 * q:32 * q + 4, :, :].bitcast(I32),
+                              in_=w4_scales[:, 4 * q:4 * q + 4, :].rearrange("a r c -> r a c").bitcast(I32))
 
-        w4_c = held([P, 2, 2 * H], U8, "w4_c")
-        nc.vector.tensor_copy(
-            out=w4_c[:].bitcast(U16).rearrange("p a (b t m) -> p (a b) t m", b=2, t=PACK),
-            in_=w4_raw[:].bitcast(U16).rearrange("p a (b m t) -> p (a b) t m", b=2, t=PACK))
+        w4_c = [held([P, 2 * H], U8, "w4_c%d" % a) for a in range(2)]
+        for a in range(2):
+            nc.vector.tensor_copy(
+                out=w4_c[a][:].bitcast(U16).rearrange("p (b t m) -> p b t m", b=2, t=PACK),
+                in_=w4_raw[a][:].bitcast(U16).rearrange("p (b m t) -> p b t m", b=2, t=PACK))
+        tab_w = [load_words(tab_words[0], "tab_w0", 0), None, None]
+        tab2_s = staged([P, T3], U8, "tab2_s", 3 * REGION)
+        nc.vector.memset(tab2_s[:].bitcast(I32), 0)
+        load_scale_rows(tab2_s, 0, tab2_scales)
 
-        v_s = held([P, S], U8, "v_s")
-        nc.vector.tensor_copy(out=v_s[:], in_=tab_s[:].indirect(offs_t[:]))
-        for a in (1, 2):
-            MQ.dma_start(out=v_s_shift[a - 1][0:SHIFT_ROWS, :].bitcast(I32),
-                                in_=v_s[4 * a:4 * a + SHIFT_ROWS, :].bitcast(I32))
-        v_planes = [v_s, v_s_shift[0], v_s_shift[1]]
+        v_s_picked = held([P, S], U8, "v_s_picked")
+        nc.vector.tensor_copy(out=v_s_picked[:], in_=tab_s[:].indirect(offs_t[:]))
+        spread_scale_rows(v_s, v_s_picked, 0, 0, 2)
+        tab_w[1] = load_words(tab_words[1], "tab_w1", REGION)
+        spread_scale_rows(v_s, v_s_picked, 32, 2, 1)
 
         w4_s = held([P, 2, H], U8, "w4_s")
         nc.vector.tensor_copy(
             out=w4_s[:].rearrange("p a (b t m) -> p (a b) t m", b=2, t=PACK),
             in_=w4_s_raw[:].rearrange("p a (b m t) -> p (a b) t m", b=2, t=PACK))
 
-        v2_s = held([P, S2], U8, "v2_s")
-        nc.vector.tensor_copy(out=v2_s[:], in_=tab2_s[:].indirect(offs2_t[:]))
+        tab_w[2] = load_words(tab_words[2], "tab_w2", 2 * REGION)
+        v2_s_picked = held([P, S2], U8, "v2_s_picked")
+        nc.vector.tensor_copy(out=v2_s_picked[:], in_=tab2_s[:].indirect(offs2_t[:]))
+        spread_scale_rows(v2_s, v2_s_picked, 0, 0, 2)
 
         def grouped(h):
             return keep.tile([P, NB * PACK], BF16, name="grouped%d" % h, tag="grouped%d" % h, align_bytes=64)
@@ -147,10 +144,10 @@ def tile_list_fastener_job_looks_kernel(tc, tab_words, tab_scales, offs, w1, w4_
                 lhsT_scale = w1_s[b][:, P * i:P * (i + 1)]
             else:
                 c0 = NB * b + P * i
-                lhsT = w4_c[:, a - 1, 2 * c0:2 * (c0 + P)].bitcast(FP4X4)
+                lhsT = w4_c[a - 1][:, 2 * c0:2 * (c0 + P)].bitcast(FP4X4)
                 lhsT_scale = w4_s[:, a - 1, c0:c0 + P]
             nc.tensor.matmul_mx(out=acc[:], lhsT=lhsT, lhsT_scale=lhsT_scale, rhs=v_w[a][h][:].bitcast(FP8X4),
-                                rhs_scale=v_planes[a][:, cols], start=(a == order[0]), stop=(a == order[2]))
+                                rhs_scale=v_s[:, a, cols], start=(a == order[0]), stop=(a == order[2]))
 
         def tanh_of(acc, b):
             th = ring.tile([P, PACK, NB], F32, name="th", tag="th", bufs=3)
@@ -185,8 +182,19 @@ def tile_list_fastener_job_looks_kernel(tc, tab_words, tab_scales, offs, w1, w4_
         acc = {}
         for h in range(2):
             acc[0, h] = [bank(h, i) for i in range(PACK)]
+        tab2_w = [None, None]
         for a in range(3):
             gather_words(a)
+            if a == 0:
+                per_row = staged([P, 2, 2, PACK], F32, "per_row", 0)
+                b1_t, gain_t = per_row[:, 0, :, :], per_row[:, 1, :, :]
+                nc.sync.dma_start(out=b1_t, in_=b1.rearrange("(b p i) -> p b i", b=2, i=PACK))
+                nc.sync.dma_start(out=gain_t, in_=gain.rearrange("(b p i) -> p b i", b=2, i=PACK))
+            if a == 1:
+                w1_raw[1] = load_w1(1, staged([P, PACK, NB], F32, "w1_raw1", REGION))
+                tab2_w[0] = load_words(tab2_words[0], "tab2_w0", REGION + REGION // 2)
+            if a == 2:
+                tab2_w[1] = load_words(tab2_words[1], "tab2_w1", 2 * REGION)
             for h in range(2):
                 for i in range(PACK):
                     first_pass(acc[0, h][i], a, 0, h, i, (0, 1, 2))
@@ -200,6 +208,13 @@ def tile_list_fastener_job_looks_kernel(tc, tab_words, tab_scales, offs, w1, w4_
             for i in range(PACK):
                 for a in (1, 2, 0):
                     first_pass(acc[1, h][i], a, 1, h, i, (1, 2, 0))
+        per_job = []
+        with nc.allow_non_contiguous_dma(reason="one value a job, jobs on the partitions"):
+            for a, src in enumerate((temp, load, finish)):
+                dst = held([P, 4], F32, "per_job%d" % a, "v_w%d_1" % a)
+                nc.sync.dma_start(out=dst[:], in_=src.rearrange("(m p) -> p m", p=P))
+                per_job.append(dst)
+        temp_t, load_t, finish_t = per_job
         hb00 = apply_gain(th00, 0, 0)
         th10 = tanh_of(acc[1, 0], 1)
         hb01 = apply_gain(th01, 0, 1)
@@ -212,15 +227,15 @@ def tile_list_fastener_job_looks_kernel(tc, tab_words, tab_scales, offs, w1, w4_
             nc.vector.tensor_copy(out=v2_w[a][:], in_=tab2_w[a][:].indirect(offs2_t[:]))
 
         gather_jobs(0)
-        quantise_h(hb01, 0, 1)
         hb10 = apply_gain(th10, 1, 0)
         gather_jobs(1)
         quantise_h(hb10, 1, 0)
+        quantise_h(hb01, 0, 1)
         hb11 = apply_gain_scalar(th11, 1)
 
         def second_pass(dst, a, h, m):
             cols = slice(P * m, P * (m + 1))
-            nc.tensor.matmul_mx(out=dst[:], lhsT=v2_w[a][:, cols].bitcast(FP8X4), lhsT_scale=v2_s[4 * a:P, cols],
+            nc.tensor.matmul_mx(out=dst[:], lhsT=v2_w[a][:, cols].bitcast(FP8X4), lhsT_scale=v2_s[:, a, cols],
                                 rhs=h_c[a][h][:].bitcast(FP8X4), rhs_scale=h_s[a][h][:], start=(a == 0), stop=(a == 1))
 
         neg_temp = held([P, 4], F32, "neg_temp")

@@ -119,8 +119,8 @@ def tile_list_fastener_job_looks_kernel(tc, tab_words, tab_scales, offs, w1, w4_
         w1_s = [held([P, NB], U8, "w1_s%d" % b) for b in range(2)]
 
         def round_w1(b, copy):
-            copy(out=w1_g[b][:].rearrange("p (t m j) -> p m t j", t=PACK, j=PACK),
-                 in_=w1_raw[b][:].rearrange("p j (m t) -> p m t j", t=PACK))
+            copy(out=w1_g[b][:].rearrange("p (t m j) -> p m j t", t=PACK, j=PACK),
+                 in_=w1_raw[b][:].rearrange("p j (m t) -> p m j t", t=PACK))
 
         def quantise_w1(b):
             nc.vector.quantize_mx(out=w1_c[b][:].bitcast(FP8X4), scales=w1_s[b][:], in_=w1_g[b][:])
@@ -158,22 +158,20 @@ def tile_list_fastener_job_looks_kernel(tc, tab_words, tab_scales, offs, w1, w4_
         h_c = [[held([P, NB], U32, "h_c%d_%d" % (b, h)) for h in range(2)] for b in range(2)]
         h_s = [[held([P, NB], U8, "h_s%d_%d" % (b, h)) for h in range(2)] for b in range(2)]
 
-        def apply_gain(th, b, h):
-            hb = grouped(h)
-            nc.vector.tensor_tensor(
-                out=hb[:].rearrange("p (c u t) -> p c t u", u=2, t=PACK),
-                in0=th[:].rearrange("p t (c u) -> p c t u", u=2),
-                in1=gain_t[:, b, :].unsqueeze(1).unsqueeze(3).to_broadcast([P, NB // 2, PACK, 2]),
-                op=ALU.mult)
-            return hb
-
-        def apply_gain_scalar(th, b):
-            hp = held([P, PACK, NB], BF16, "hp")
+        def apply_gain(th, b, on_scalar):
+            hp = ring.tile([P, PACK, NB], BF16, name="hp", tag="hp")
             for i in range(PACK):
-                nc.scalar.activation(out=hp[:, i, :], in_=th[:, i, :], func=ACT.Copy, scale=gain_t[:, b, i:i + 1])
-            hb = held([P, NB * PACK], BF16, "hb_last")
-            nc.scalar.copy(out=hb[:].rearrange("p (c u t) -> p c t u", u=2, t=PACK),
-                           in_=hp[:].rearrange("p t (c u) -> p c t u", u=2))
+                if on_scalar:
+                    nc.scalar.activation(out=hp[:, i, :], in_=th[:, i, :], func=ACT.Copy, scale=gain_t[:, b, i:i + 1])
+                else:
+                    nc.vector.tensor_scalar(out=hp[:, i, :], in0=th[:, i, :], scalar1=gain_t[:, b, i:i + 1],
+                                            scalar2=None, op0=ALU.mult)
+            return hp
+
+        def interleave(hp, h):
+            hb = grouped(h)
+            nc.vector.tensor_copy(out=hb[:].rearrange("p (c u t) -> p c t u", u=4, t=PACK),
+                                  in_=hp[:].rearrange("p t (c u) -> p c t u", u=4))
             return hb
 
         def quantise_h(hb, b, h):
@@ -215,23 +213,25 @@ def tile_list_fastener_job_looks_kernel(tc, tab_words, tab_scales, offs, w1, w4_
                 nc.sync.dma_start(out=dst[:], in_=src.rearrange("(m p) -> p m", p=P))
                 per_job.append(dst)
         temp_t, load_t, finish_t = per_job
-        hb00 = apply_gain(th00, 0, 0)
-        th10 = tanh_of(acc[1, 0], 1)
-        hb01 = apply_gain(th01, 0, 1)
-        quantise_h(hb00, 0, 0)
-        th11 = tanh_of(acc[1, 1], 1)
-
         v2_w = [held([P, S2], U32, "v2_w%d" % a) for a in range(2)]
 
         def gather_jobs(a):
             nc.vector.tensor_copy(out=v2_w[a][:], in_=tab2_w[a][:].indirect(offs2_t[:]))
 
+        hp00 = apply_gain(th00, 0, False)
+        th10 = tanh_of(acc[1, 0], 1)
+        hb00 = interleave(hp00, 0)
+        hp01 = apply_gain(th01, 0, False)
+        quantise_h(hb00, 0, 0)
+        hb01 = interleave(hp01, 1)
+        hp10 = apply_gain(th10, 1, True)
+        th11 = tanh_of(acc[1, 1], 1)
+        hp11 = apply_gain(th11, 1, True)
         gather_jobs(0)
-        hb10 = apply_gain(th10, 1, 0)
         gather_jobs(1)
-        quantise_h(hb10, 1, 0)
+        hb10 = interleave(hp10, 0)
         quantise_h(hb01, 0, 1)
-        hb11 = apply_gain_scalar(th11, 1)
+        quantise_h(hb10, 1, 0)
 
         def second_pass(dst, a, h, m):
             cols = slice(P * m, P * (m + 1))
@@ -259,8 +259,10 @@ def tile_list_fastener_job_looks_kernel(tc, tab_words, tab_scales, offs, w1, w4_
                                     scalar2=(None if h == 0 else top_half[:, m:m + 1]), op0=ALU.mult, op1=ALU.max,
                                     accum_out=(top_half if h == 0 else top)[:, m:m + 1])
 
-        for m in range(3):
+        for m in range(2):
             scores_out(0, m)
+        hb11 = interleave(hp11, 1)
+        scores_out(0, 2)
         quantise_h(hb11, 1, 1)
         for m in range(4):
             second_pass(sc[1][m], 1, 1, m)

@@ -37,28 +37,32 @@ def tile_list_fastener_job_looks_kernel(tc, tab_words, tab_scales, offs, w1, w4_
         def staged(shape, dtype, name, offset):
             return stage.tile(shape, dtype, name=name, align_bytes=64, offset=offset)
 
-        REGION = 4 * T
         offs_t = lists.tile([P, S // 16], U16, name="offs_t")
         offs2_t = lists.tile([P, S2 // 16], U16, name="offs2_t")
         pos1_t = lists.tile([P, NP // 16], U16, name="pos1_t")
         pos2_t = lists.tile([P, NP // 16], U16, name="pos2_t")
 
-        tab_s = staged([P, T], U8, "tab_s", REGION)
-        w4_s_raw = staged([P, 2, H], U8, "w4_s_raw", 2 * REGION)
-        v_s = held([P, 3, S], U8, "v_s")
+        KB1 = 1024
+        w4_s_raw = held([P, 2, H], U8, "w4_s_raw")
+        nc.vector.memset(w4_s_raw[:].rearrange("p a c -> p (a c)").bitcast(I32), 0)
+        tab_s = staged([P, T], U8, "tab_s", 7 * KB1)
+        tab2_s = staged([P, T3], U8, "tab2_s", 33 * KB1)
+        w4_raw = staged([P, 2, 2 * H], U8, "w4_raw", 49 * KB1)
+        v_s12 = held([P, 2, S], U8, "v_s12")
+        v_s0 = held([P, 1, S], U8, "v_s0")
         v2_s = held([P, 2, S2], U8, "v2_s")
-        nc.vector.memset(tab_s[:].bitcast(I32), 0)
-        for t in (w4_s_raw, v_s, v2_s):
+        nc.vector.memset(tab_s[32:64, :].bitcast(I32), 0)
+        nc.vector.memset(tab_s[64:112, :].bitcast(I32), 0)
+        nc.gpsimd.memset(tab2_s[0:64, :].bitcast(I32), 0)
+        nc.gpsimd.memset(tab2_s[96:128, :].bitcast(I32), 0)
+        for t in (v_s12, v_s0, v2_s):
             nc.vector.memset(t[:].rearrange("p a c -> p (a c)").bitcast(I32), 0)
-
-        w4_raw = [staged([P, 2 * H], U8, "w4_raw%d" % a, 3 * a * REGION) for a in range(2)]
 
         def load_w1(b, raw):
             nc.sync.dma_start(out=raw[:], in_=w1[:, NB * b:NB * (b + 1)].rearrange("(p j) c -> p j c", j=PACK))
             return raw
 
-        def load_words(src, name, offset):
-            dst = staged([P, src.shape[1]], U32, name, offset)
+        def load_words(src, dst):
             nc.sync.dma_start(out=dst[:].bitcast(I32), in_=src.rearrange("p t i -> p (t i)").bitcast(I32))
             return dst
 
@@ -67,49 +71,53 @@ def tile_list_fastener_job_looks_kernel(tc, tab_words, tab_scales, offs, w1, w4_
             nc.sync.dma_start(out=dst[row0:row0 + rows, :].bitcast(I32),
                               in_=src.rearrange("a q c -> q a c").bitcast(I32))
 
-        def spread_scale_rows(planes, picked, row0, first, passes):
+        def spread_scale_rows(planes, k0, picked, row0):
+            passes = planes.shape[1]
             for q in range(4):
-                nc.sync.dma_start(out=planes[32 * q:32 * q + 4, first:first + passes, :].bitcast(I32),
+                nc.sync.dma_start(out=planes[32 * q + k0:32 * q + k0 + 4, :, :].bitcast(I32),
                                   in_=picked[row0 + 4 * passes * q:row0 + 4 * passes * (q + 1), :].bitcast(I32))
 
-        nc.sync.dma_start(out=w4_raw[0][:].bitcast(I32), in_=w4_words[0].bitcast(I32))
+        tab_w = [None, None, None]
         nc.sync.dma_start(offs_t[:], offs)
+        load_scale_rows(tab_s, 0, tab_scales[1:3])
+        load_scale_rows(tab_s, 112, tab_scales[0:1])
         nc.sync.dma_start(offs2_t[:], offs2)
+        load_scale_rows(tab2_s, 64, tab2_scales)
+        nc.sync.dma_start(out=w4_raw[:].bitcast(I32), in_=w4_words.rearrange("a p n -> p a n").bitcast(I32))
+        tab_w[1] = load_words(tab_words[1], held([P, T], U32, "tab_w1"))
         nc.sync.dma_start(pos1_t[:], pos1)
         nc.sync.dma_start(pos2_t[:], pos2)
-        nc.sync.dma_start(out=w4_raw[1][:].bitcast(I32), in_=w4_words[1].bitcast(I32))
-        w1_raw = [load_w1(0, held([P, PACK, NB], F32, "w1_raw0")), None]
-        load_scale_rows(tab_s, 0, tab_scales[0:2])
-        load_scale_rows(tab_s, 32, tab_scales[2:3])
         for q in range(4):
             nc.sync.dma_start(out=w4_s_raw[32 * q:32 * q + 4, :, :].bitcast(I32),
                               in_=w4_scales[:, 4 * q:4 * q + 4, :].rearrange("a r c -> r a c").bitcast(I32))
-
-        w4_c = [held([P, 2 * H], U8, "w4_c%d" % a) for a in range(2)]
-        for a in range(2):
-            nc.vector.tensor_copy(
-                out=w4_c[a][:].bitcast(U16).rearrange("p (b t m) -> p b t m", b=2, t=PACK),
-                in_=w4_raw[a][:].bitcast(U16).rearrange("p (b m t) -> p b t m", b=2, t=PACK))
-        tab_w = [load_words(tab_words[0], "tab_w0", 0), None, None]
-        tab2_s = staged([P, T3], U8, "tab2_s", 3 * REGION)
-        nc.vector.memset(tab2_s[:].bitcast(I32), 0)
-        load_scale_rows(tab2_s, 0, tab2_scales)
+        tab_w[2] = load_words(tab_words[2], held([P, T], U32, "tab_w2"))
 
         v_s_picked = held([P, S], U8, "v_s_picked")
         nc.vector.tensor_copy(out=v_s_picked[:], in_=tab_s[:].indirect(offs_t[:]))
-        spread_scale_rows(v_s, v_s_picked, 0, 0, 2)
-        tab_w[1] = load_words(tab_words[1], "tab_w1", REGION)
-        spread_scale_rows(v_s, v_s_picked, 32, 2, 1)
+        spread_scale_rows(v_s12, 0, v_s_picked, 0)
+        w1_raw = [load_w1(0, staged([P, PACK, NB], F32, "w1_raw0", 0)), None]
+        tab_w[0] = load_words(tab_words[0], staged([P, T], U32, "tab_w0", 10 * KB1))
+        spread_scale_rows(v_s0, 4, v_s_picked, 112)
+        per_row = staged([P, 2, 2, PACK], F32, "per_row", 9 * KB1)
+        b1_t, gain_t = per_row[:, 0, :, :], per_row[:, 1, :, :]
+        nc.sync.dma_start(out=b1_t, in_=b1.rearrange("(b p i) -> p b i", b=2, i=PACK))
+        nc.sync.dma_start(out=gain_t, in_=gain.rearrange("(b p i) -> p b i", b=2, i=PACK))
+
+        w4_c = held([P, 2, 2 * H], U8, "w4_c")
+        nc.vector.tensor_copy(
+            out=w4_c[:].bitcast(U16).rearrange("p a (b t m) -> p (a b) t m", b=2, t=PACK),
+            in_=w4_raw[:].bitcast(U16).rearrange("p a (b m t) -> p (a b) t m", b=2, t=PACK))
+        w1_raw[1] = load_w1(1, staged([P, PACK, NB], F32, "w1_raw1", 42 * KB1))
+
+        v2_s_picked = staged([P, S2], U8, "v2_s_picked", 52 * KB1 + 512)
+        nc.vector.tensor_copy(out=v2_s_picked[:], in_=tab2_s[:].indirect(offs2_t[:]))
+        tab2_w = [load_words(tab2_words[a], staged([P, T3], U32, "tab2_w%d" % a, (26 + 8 * a) * KB1)) for a in range(2)]
+        spread_scale_rows(v2_s, 8, v2_s_picked, 64)
 
         w4_s = held([P, 2, H], U8, "w4_s")
         nc.vector.tensor_copy(
             out=w4_s[:].rearrange("p a (b t m) -> p (a b) t m", b=2, t=PACK),
             in_=w4_s_raw[:].rearrange("p a (b m t) -> p (a b) t m", b=2, t=PACK))
-
-        tab_w[2] = load_words(tab_words[2], "tab_w2", 2 * REGION)
-        v2_s_picked = held([P, S2], U8, "v2_s_picked")
-        nc.vector.tensor_copy(out=v2_s_picked[:], in_=tab2_s[:].indirect(offs2_t[:]))
-        spread_scale_rows(v2_s, v2_s_picked, 0, 0, 2)
 
         def grouped(h):
             return keep.tile([P, NB * PACK], BF16, name="grouped%d" % h, tag="grouped%d" % h, align_bytes=64)
@@ -119,14 +127,11 @@ def tile_list_fastener_job_looks_kernel(tc, tab_words, tab_scales, offs, w1, w4_
         w1_s = [held([P, NB], U8, "w1_s%d" % b) for b in range(2)]
 
         def round_w1(b, copy):
-            copy(out=w1_g[b][:].rearrange("p (t m j) -> p m j t", t=PACK, j=PACK),
-                 in_=w1_raw[b][:].rearrange("p j (m t) -> p m j t", t=PACK))
+            copy(out=w1_g[b][:].rearrange("p (t m j) -> p m t j", t=PACK, j=PACK),
+                 in_=w1_raw[b][:].rearrange("p j (m t) -> p m t j", t=PACK))
 
         def quantise_w1(b):
             nc.vector.quantize_mx(out=w1_c[b][:].bitcast(FP8X4), scales=w1_s[b][:], in_=w1_g[b][:])
-
-        round_w1(0, nc.scalar.copy)
-        quantise_w1(0)
 
         v_w = [[held([P, NB], U32, "v_w%d_%d" % (a, h)) for h in range(2)] for a in range(3)]
 
@@ -142,12 +147,14 @@ def tile_list_fastener_job_looks_kernel(tc, tab_words, tab_scales, offs, w1, w4_
             if a == 0:
                 lhsT = w1_c[b][:, P * i:P * (i + 1)].bitcast(FP8X4)
                 lhsT_scale = w1_s[b][:, P * i:P * (i + 1)]
+                rhs_scale = v_s0[4:P, 0, cols]
             else:
                 c0 = NB * b + P * i
-                lhsT = w4_c[a - 1][:, 2 * c0:2 * (c0 + P)].bitcast(FP4X4)
+                lhsT = w4_c[:, a - 1, 2 * c0:2 * (c0 + P)].bitcast(FP4X4)
                 lhsT_scale = w4_s[:, a - 1, c0:c0 + P]
+                rhs_scale = v_s12[:, a - 1, cols]
             nc.tensor.matmul_mx(out=acc[:], lhsT=lhsT, lhsT_scale=lhsT_scale, rhs=v_w[a][h][:].bitcast(FP8X4),
-                                rhs_scale=v_s[:, a, cols], start=(a == order[0]), stop=(a == order[2]))
+                                rhs_scale=rhs_scale, start=(a == order[0]), stop=(a == order[2]))
 
         def tanh_of(acc, b):
             th = ring.tile([P, PACK, NB], F32, name="th", tag="th", bufs=3)
@@ -158,20 +165,22 @@ def tile_list_fastener_job_looks_kernel(tc, tab_words, tab_scales, offs, w1, w4_
         h_c = [[held([P, NB], U32, "h_c%d_%d" % (b, h)) for h in range(2)] for b in range(2)]
         h_s = [[held([P, NB], U8, "h_s%d_%d" % (b, h)) for h in range(2)] for b in range(2)]
 
-        def apply_gain(th, b, on_scalar):
-            hp = ring.tile([P, PACK, NB], BF16, name="hp", tag="hp")
-            for i in range(PACK):
-                if on_scalar:
-                    nc.scalar.activation(out=hp[:, i, :], in_=th[:, i, :], func=ACT.Copy, scale=gain_t[:, b, i:i + 1])
-                else:
-                    nc.vector.tensor_scalar(out=hp[:, i, :], in0=th[:, i, :], scalar1=gain_t[:, b, i:i + 1],
-                                            scalar2=None, op0=ALU.mult)
-            return hp
-
-        def interleave(hp, h):
+        def apply_gain(th, b, h):
             hb = grouped(h)
-            nc.vector.tensor_copy(out=hb[:].rearrange("p (c u t) -> p c t u", u=4, t=PACK),
-                                  in_=hp[:].rearrange("p t (c u) -> p c t u", u=4))
+            nc.vector.tensor_tensor(
+                out=hb[:].rearrange("p (c u t) -> p c t u", u=2, t=PACK),
+                in0=th[:].rearrange("p t (c u) -> p c t u", u=2),
+                in1=gain_t[:, b, :].unsqueeze(1).unsqueeze(3).to_broadcast([P, NB // 2, PACK, 2]),
+                op=ALU.mult)
+            return hb
+
+        def apply_gain_scalar(th, b):
+            hp = held([P, PACK, NB], BF16, "hp")
+            for i in range(PACK):
+                nc.scalar.activation(out=hp[:, i, :], in_=th[:, i, :], func=ACT.Copy, scale=gain_t[:, b, i:i + 1])
+            hb = held([P, NB * PACK], BF16, "hb_last")
+            nc.scalar.copy(out=hb[:].rearrange("p (c u t) -> p c t u", u=2, t=PACK),
+                           in_=hp[:].rearrange("p t (c u) -> p c t u", u=2))
             return hb
 
         def quantise_h(hb, b, h):
@@ -180,22 +189,14 @@ def tile_list_fastener_job_looks_kernel(tc, tab_words, tab_scales, offs, w1, w4_
         acc = {}
         for h in range(2):
             acc[0, h] = [bank(h, i) for i in range(PACK)]
-        tab2_w = [None, None]
-        for a in range(3):
-            gather_words(a)
+        for a in (1, 2, 0):
             if a == 0:
-                per_row = staged([P, 2, 2, PACK], F32, "per_row", 0)
-                b1_t, gain_t = per_row[:, 0, :, :], per_row[:, 1, :, :]
-                nc.sync.dma_start(out=b1_t, in_=b1.rearrange("(b p i) -> p b i", b=2, i=PACK))
-                nc.sync.dma_start(out=gain_t, in_=gain.rearrange("(b p i) -> p b i", b=2, i=PACK))
-            if a == 1:
-                w1_raw[1] = load_w1(1, staged([P, PACK, NB], F32, "w1_raw1", REGION))
-                tab2_w[0] = load_words(tab2_words[0], "tab2_w0", REGION + REGION // 2)
-            if a == 2:
-                tab2_w[1] = load_words(tab2_words[1], "tab2_w1", 2 * REGION)
+                round_w1(0, nc.scalar.copy)
+                quantise_w1(0)
+            gather_words(a)
             for h in range(2):
                 for i in range(PACK):
-                    first_pass(acc[0, h][i], a, 0, h, i, (0, 1, 2))
+                    first_pass(acc[0, h][i], a, 0, h, i, (1, 2, 0))
 
         round_w1(1, nc.vector.tensor_copy)
         th00 = tanh_of(acc[0, 0], 0)
@@ -213,29 +214,27 @@ def tile_list_fastener_job_looks_kernel(tc, tab_words, tab_scales, offs, w1, w4_
                 nc.sync.dma_start(out=dst[:], in_=src.rearrange("(m p) -> p m", p=P))
                 per_job.append(dst)
         temp_t, load_t, finish_t = per_job
+        hb00 = apply_gain(th00, 0, 0)
+        th10 = tanh_of(acc[1, 0], 1)
+        hb01 = apply_gain(th01, 0, 1)
+        quantise_h(hb00, 0, 0)
+        th11 = tanh_of(acc[1, 1], 1)
+
         v2_w = [held([P, S2], U32, "v2_w%d" % a) for a in range(2)]
 
         def gather_jobs(a):
             nc.vector.tensor_copy(out=v2_w[a][:], in_=tab2_w[a][:].indirect(offs2_t[:]))
 
-        hp00 = apply_gain(th00, 0, False)
-        th10 = tanh_of(acc[1, 0], 1)
-        hb00 = interleave(hp00, 0)
-        hp01 = apply_gain(th01, 0, False)
-        quantise_h(hb00, 0, 0)
-        hb01 = interleave(hp01, 1)
-        hp10 = apply_gain(th10, 1, True)
-        th11 = tanh_of(acc[1, 1], 1)
-        hp11 = apply_gain(th11, 1, True)
         gather_jobs(0)
+        hb10 = apply_gain(th10, 1, 0)
         gather_jobs(1)
-        hb10 = interleave(hp10, 0)
-        quantise_h(hb01, 0, 1)
         quantise_h(hb10, 1, 0)
+        quantise_h(hb01, 0, 1)
+        hb11 = apply_gain_scalar(th11, 1)
 
         def second_pass(dst, a, h, m):
             cols = slice(P * m, P * (m + 1))
-            nc.tensor.matmul_mx(out=dst[:], lhsT=v2_w[a][:, cols].bitcast(FP8X4), lhsT_scale=v2_s[:, a, cols],
+            nc.tensor.matmul_mx(out=dst[:], lhsT=v2_w[a][:, cols].bitcast(FP8X4), lhsT_scale=v2_s[8:P, a, cols],
                                 rhs=h_c[a][h][:].bitcast(FP8X4), rhs_scale=h_s[a][h][:], start=(a == 0), stop=(a == 1))
 
         neg_temp = held([P, 4], F32, "neg_temp")
@@ -259,10 +258,8 @@ def tile_list_fastener_job_looks_kernel(tc, tab_words, tab_scales, offs, w1, w4_
                                     scalar2=(None if h == 0 else top_half[:, m:m + 1]), op0=ALU.mult, op1=ALU.max,
                                     accum_out=(top_half if h == 0 else top)[:, m:m + 1])
 
-        for m in range(2):
+        for m in range(3):
             scores_out(0, m)
-        hb11 = interleave(hp11, 1)
-        scores_out(0, 2)
         quantise_h(hb11, 1, 1)
         for m in range(4):
             second_pass(sc[1][m], 1, 1, m)

@@ -2,7 +2,7 @@ from contextlib import ExitStack
 
 import concourse.mybir as mybir
 
-T, S, K, KA, KB, H, T3, S2, NP = 4096, 1024, 1536, 512, 1024, 1024, 2048, 512, 512
+T, S, K, H, T3, S2, NP = 4096, 1024, 1536, 1024, 2048, 512, 512
 FLOPS = 2 * K * H * S + 2 * H * S2 * S
 
 F32 = mybir.dt.float32
@@ -19,6 +19,13 @@ ACT = mybir.ActivationFunctionType
 P = 128
 PACK = 4
 NB = 512
+JOB_TILES = S2 // P
+KIB = 1024
+PASS_ORDER = (1, 2, 0)
+WALK = 4
+SPLIT = 384
+TAB_ROWS_12, TAB_ROWS_0, TAB2_ROWS = 0, 112, 64
+PLANE_V0, PLANE_V2 = 4, 8
 
 
 def tile_list_fastener_job_looks_kernel(tc, tab_words, tab_scales, offs, w1, w4_words, w4_scales, b1, gain,
@@ -42,21 +49,20 @@ def tile_list_fastener_job_looks_kernel(tc, tab_words, tab_scales, offs, w1, w4_
         pos1_t = lists.tile([P, NP // 16], U16, name="pos1_t")
         pos2_t = lists.tile([P, NP // 16], U16, name="pos2_t")
 
-        KB1 = 1024
         w4_s_raw = held([P, 2, H], U8, "w4_s_raw")
         nc.vector.memset(w4_s_raw[:].rearrange("p a c -> p (a c)").bitcast(I32), 0)
-        tab_s = staged([P, T], U8, "tab_s", 7 * KB1)
-        tab2_s = staged([P, T3], U8, "tab2_s", 33 * KB1)
-        w4_raw = staged([P, 2, 2 * H], U8, "w4_raw", 49 * KB1)
+        tab_s = staged([P, T], U8, "tab_s", 7 * KIB)
+        tab2_s = staged([P, T3], U8, "tab2_s", 33 * KIB)
+        w4_raw = staged([P, 2, 2 * H], U8, "w4_raw", 49 * KIB)
         v_s12 = held([P, 2, S], U8, "v_s12")
         v_s0 = held([P, 1, S], U8, "v_s0")
         v2_s = held([P, 2, S2], U8, "v2_s")
         nc.vector.memset(tab_s[32:64, :].bitcast(I32), 0)
-        nc.vector.memset(tab_s[64:112, :].bitcast(I32), 0)
-        nc.gpsimd.memset(tab2_s[0:64, :].bitcast(I32), 0)
-        nc.gpsimd.memset(tab2_s[96:128, :].bitcast(I32), 0)
-        for t in (v_s12, v_s0, v2_s):
-            nc.vector.memset(t[:].rearrange("p a c -> p (a c)").bitcast(I32), 0)
+        nc.vector.memset(tab_s[64:TAB_ROWS_0, :].bitcast(I32), 0)
+        nc.gpsimd.memset(tab2_s[0:TAB2_ROWS, :].bitcast(I32), 0)
+        nc.gpsimd.memset(tab2_s[96:P, :].bitcast(I32), 0)
+        for planes in (v_s12, v_s0, v2_s):
+            nc.vector.memset(planes[:].rearrange("p a c -> p (a c)").bitcast(I32), 0)
 
         def load_w1(b, raw):
             nc.sync.dma_start(out=raw[:], in_=w1[:, NB * b:NB * (b + 1)].rearrange("(p j) c -> p j c", j=PACK))
@@ -69,20 +75,20 @@ def tile_list_fastener_job_looks_kernel(tc, tab_words, tab_scales, offs, w1, w4_
         def load_scale_rows(dst, row0, src):
             rows = src.shape[0] * src.shape[1]
             nc.sync.dma_start(out=dst[row0:row0 + rows, :].bitcast(I32),
-                              in_=src.rearrange("a q c -> q a c").bitcast(I32))
+                              in_=src.rearrange("a g c -> g a c").bitcast(I32))
 
-        def spread_scale_rows(planes, k0, picked, row0):
+        def spread_scale_rows(planes, first, gathered, row0):
             passes = planes.shape[1]
             for q in range(4):
-                nc.sync.dma_start(out=planes[32 * q + k0:32 * q + k0 + 4, :, :].bitcast(I32),
-                                  in_=picked[row0 + 4 * passes * q:row0 + 4 * passes * (q + 1), :].bitcast(I32))
+                nc.sync.dma_start(out=planes[32 * q + first:32 * q + first + 4, :, :].bitcast(I32),
+                                  in_=gathered[row0 + 4 * passes * q:row0 + 4 * passes * (q + 1), :].bitcast(I32))
 
         tab_w = [None, None, None]
         nc.sync.dma_start(offs_t[:], offs)
-        load_scale_rows(tab_s, 0, tab_scales[1:3])
-        load_scale_rows(tab_s, 112, tab_scales[0:1])
+        load_scale_rows(tab_s, TAB_ROWS_12, tab_scales[1:3])
+        load_scale_rows(tab_s, TAB_ROWS_0, tab_scales[0:1])
         nc.sync.dma_start(offs2_t[:], offs2)
-        load_scale_rows(tab2_s, 64, tab2_scales)
+        load_scale_rows(tab2_s, TAB2_ROWS, tab2_scales)
         nc.sync.dma_start(out=w4_raw[:].bitcast(I32), in_=w4_words.rearrange("a p n -> p a n").bitcast(I32))
         tab_w[1] = load_words(tab_words[1], held([P, T], U32, "tab_w1"))
         nc.sync.dma_start(pos1_t[:], pos1)
@@ -94,176 +100,183 @@ def tile_list_fastener_job_looks_kernel(tc, tab_words, tab_scales, offs, w1, w4_
 
         v_s_picked = held([P, S], U8, "v_s_picked")
         nc.vector.tensor_copy(out=v_s_picked[:], in_=tab_s[:].indirect(offs_t[:]))
-        spread_scale_rows(v_s12, 0, v_s_picked, 0)
+        spread_scale_rows(v_s12, 0, v_s_picked, TAB_ROWS_12)
         w1_raw = [load_w1(0, staged([P, PACK, NB], F32, "w1_raw0", 0)), None]
-        tab_w[0] = load_words(tab_words[0], staged([P, T], U32, "tab_w0", 10 * KB1))
-        spread_scale_rows(v_s0, 4, v_s_picked, 112)
-        per_row = staged([P, 2, 2, PACK], F32, "per_row", 9 * KB1)
+        tab_w[0] = load_words(tab_words[0], staged([P, T], U32, "tab_w0", 10 * KIB))
+        spread_scale_rows(v_s0, PLANE_V0, v_s_picked, TAB_ROWS_0)
+        per_row = staged([P, 2, 2, PACK], F32, "per_row", 9 * KIB)
         b1_t, gain_t = per_row[:, 0, :, :], per_row[:, 1, :, :]
         nc.sync.dma_start(out=b1_t, in_=b1.rearrange("(b p i) -> p b i", b=2, i=PACK))
         nc.sync.dma_start(out=gain_t, in_=gain.rearrange("(b p i) -> p b i", b=2, i=PACK))
 
         w4_c = held([P, 2, 2 * H], U8, "w4_c")
         nc.vector.tensor_copy(
-            out=w4_c[:].bitcast(U16).rearrange("p a (b t m) -> p (a b) t m", b=2, t=PACK),
-            in_=w4_raw[:].bitcast(U16).rearrange("p a (b m t) -> p (a b) t m", b=2, t=PACK))
-        w1_raw[1] = load_w1(1, staged([P, PACK, NB], F32, "w1_raw1", 42 * KB1))
+            out=w4_c[:].bitcast(U16).rearrange("p a (b i m) -> p (a b) i m", b=2, i=PACK),
+            in_=w4_raw[:].bitcast(U16).rearrange("p a (b m i) -> p (a b) i m", b=2, i=PACK))
+        w1_raw[1] = load_w1(1, staged([P, PACK, NB], F32, "w1_raw1", 42 * KIB))
 
-        v2_s_picked = staged([P, S2], U8, "v2_s_picked", 52 * KB1 + 512)
+        v2_s_picked = staged([P, S2], U8, "v2_s_picked", 53 * KIB - S2)
         nc.vector.tensor_copy(out=v2_s_picked[:], in_=tab2_s[:].indirect(offs2_t[:]))
-        tab2_w = [load_words(tab2_words[a], staged([P, T3], U32, "tab2_w%d" % a, (26 + 8 * a) * KB1)) for a in range(2)]
-        spread_scale_rows(v2_s, 8, v2_s_picked, 64)
+        tab2_w = [load_words(tab2_words[a], staged([P, T3], U32, "tab2_w%d" % a, (26 + 8 * a) * KIB)) for a in range(2)]
+        spread_scale_rows(v2_s, PLANE_V2, v2_s_picked, TAB2_ROWS)
 
         w4_s = held([P, 2, H], U8, "w4_s")
         nc.vector.tensor_copy(
-            out=w4_s[:].rearrange("p a (b t m) -> p (a b) t m", b=2, t=PACK),
-            in_=w4_s_raw[:].rearrange("p a (b m t) -> p (a b) t m", b=2, t=PACK))
+            out=w4_s[:].rearrange("p a (b i m) -> p (a b) i m", b=2, i=PACK),
+            in_=w4_s_raw[:].rearrange("p a (b m i) -> p (a b) i m", b=2, i=PACK))
 
-        def grouped(h):
-            return keep.tile([P, NB * PACK], BF16, name="grouped%d" % h, tag="grouped%d" % h, align_bytes=64)
+        def grouped(slot):
+            return keep.tile([P, NB * PACK], BF16, name="grouped%d" % slot, tag="grouped%d" % slot, align_bytes=64)
 
         w1_g = [grouped(1), grouped(0)]
         w1_c = [held([P, NB], U32, "w1_c%d" % b) for b in range(2)]
         w1_s = [held([P, NB], U8, "w1_s%d" % b) for b in range(2)]
 
         def round_w1(b, copy):
-            copy(out=w1_g[b][:].rearrange("p (t m j) -> p m t j", t=PACK, j=PACK),
-                 in_=w1_raw[b][:].rearrange("p j (m t) -> p m t j", t=PACK))
+            copy(out=w1_g[b][:].rearrange("p (i m j) -> p m i j", i=PACK, j=PACK),
+                 in_=w1_raw[b][:].rearrange("p j (m i) -> p m i j", i=PACK))
 
         def quantise_w1(b):
             nc.vector.quantize_mx(out=w1_c[b][:].bitcast(FP8X4), scales=w1_s[b][:], in_=w1_g[b][:])
 
-        v_w = [[held([P, NB], U32, "v_w%d_%d" % (a, h)) for h in range(2)] for a in range(3)]
+        v_w = [[held([P, NB], U32, "v_w%d_%d" % (a, half)) for half in range(2)] for a in range(3)]
 
         def gather_words(a):
-            for h in range(2):
-                nc.vector.tensor_copy(out=v_w[a][h][:], in_=tab_w[a][:].indirect(offs_t[:, 32 * h:32 * (h + 1)]))
+            for half in range(2):
+                nc.vector.tensor_copy(out=v_w[a][half][:],
+                                      in_=tab_w[a][:].indirect(offs_t[:, 32 * half:32 * (half + 1)]))
 
-        def bank(h, i):
-            return psum.tile([P, NB], F32, name="bank%d_%d" % (h, i), tag="bank%d_%d" % (h, i))
+        def bank(half, n):
+            return psum.tile([P, NB], F32, name="bank%d_%d" % (half, n), tag="bank%d_%d" % (half, n))
 
-        def first_pass(acc, a, b, h, i, order):
-            cols = slice(NB * h, NB * (h + 1))
+        def first_pass(dst, a, b, half, i):
+            cols = slice(NB * half, NB * (half + 1))
             if a == 0:
                 lhsT = w1_c[b][:, P * i:P * (i + 1)].bitcast(FP8X4)
                 lhsT_scale = w1_s[b][:, P * i:P * (i + 1)]
-                rhs_scale = v_s0[4:P, 0, cols]
+                rhs_scale = v_s0[PLANE_V0:P, 0, cols]
             else:
                 c0 = NB * b + P * i
                 lhsT = w4_c[:, a - 1, 2 * c0:2 * (c0 + P)].bitcast(FP4X4)
                 lhsT_scale = w4_s[:, a - 1, c0:c0 + P]
                 rhs_scale = v_s12[:, a - 1, cols]
-            nc.tensor.matmul_mx(out=acc[:], lhsT=lhsT, lhsT_scale=lhsT_scale, rhs=v_w[a][h][:].bitcast(FP8X4),
-                                rhs_scale=rhs_scale, start=(a == order[0]), stop=(a == order[2]))
+            nc.tensor.matmul_mx(out=dst[:], lhsT=lhsT, lhsT_scale=lhsT_scale, rhs=v_w[a][half][:].bitcast(FP8X4),
+                                rhs_scale=rhs_scale, start=(a == PASS_ORDER[0]), stop=(a == PASS_ORDER[2]))
 
-        def tanh_of(acc, b):
+        def tanh_of(banks, b):
             th = ring.tile([P, PACK, NB], F32, name="th", tag="th", bufs=3)
             for i in range(PACK):
-                nc.scalar.activation(out=th[:, i, :], in_=acc[i][:], func=ACT.Tanh, bias=b1_t[:, b, i:i + 1])
+                nc.scalar.activation(out=th[:, i, :], in_=banks[i][:], func=ACT.Tanh, bias=b1_t[:, b, i:i + 1])
             return th
 
-        h_c = [[held([P, NB], U32, "h_c%d_%d" % (b, h)) for h in range(2)] for b in range(2)]
-        h_s = [[held([P, NB], U8, "h_s%d_%d" % (b, h)) for h in range(2)] for b in range(2)]
+        h_c, h_s = {}, {}
 
-        def apply_gain(th, b, h):
-            hb = grouped(h)
+        def gain_and_weave(th, b, half):
+            hb = grouped(half)
             nc.vector.tensor_tensor(
-                out=hb[:].rearrange("p (c u t) -> p c t u", u=2, t=PACK),
-                in0=th[:].rearrange("p t (c u) -> p c t u", u=2),
-                in1=gain_t[:, b, :].unsqueeze(1).unsqueeze(3).to_broadcast([P, NB // 2, PACK, 2]),
+                out=hb[:].rearrange("p (c u i) -> p c i u", u=WALK, i=PACK),
+                in0=th[:].rearrange("p i (c u) -> p c i u", u=WALK),
+                in1=gain_t[:, b, :].unsqueeze(1).unsqueeze(3).to_broadcast([P, NB // WALK, PACK, WALK]),
                 op=ALU.mult)
             return hb
 
-        def apply_gain_scalar(th, b):
-            hp = held([P, PACK, NB], BF16, "hp")
+        def gain_planes(th, b, half):
+            hp = held([P, PACK, NB], BF16, "hp%d" % half)
             for i in range(PACK):
                 nc.scalar.activation(out=hp[:, i, :], in_=th[:, i, :], func=ACT.Copy, scale=gain_t[:, b, i:i + 1])
-            hb = held([P, NB * PACK], BF16, "hb_last")
-            nc.scalar.copy(out=hb[:].rearrange("p (c u t) -> p c t u", u=2, t=PACK),
-                           in_=hp[:].rearrange("p t (c u) -> p c t u", u=2))
-            return hb
+            return hp
 
-        def quantise_h(hb, b, h):
-            nc.vector.quantize_mx(out=h_c[b][h][:].bitcast(FP8X4), scales=h_s[b][h][:], in_=hb[:])
+        def weave(copy, hb, hp, c0, c1):
+            copy(out=hb[:, PACK * c0:PACK * c1].rearrange("p (c u i) -> p c i u", u=WALK, i=PACK),
+                 in_=hp[:, :, c0:c1].rearrange("p i (c u) -> p c i u", u=WALK))
 
-        acc = {}
-        for h in range(2):
-            acc[0, h] = [bank(h, i) for i in range(PACK)]
-        for a in (1, 2, 0):
+        def quantise_h(hb, b, half, after=None):
+            h_c[b, half] = held([P, NB], U32, "h_c%d_%d" % (b, half), after)
+            h_s[b, half] = held([P, NB], U8, "h_s%d_%d" % (b, half))
+            nc.vector.quantize_mx(out=h_c[b, half][:].bitcast(FP8X4), scales=h_s[b, half][:], in_=hb[:])
+
+        f_banks = {}
+        for half in range(2):
+            f_banks[0, half] = [bank(half, i) for i in range(PACK)]
+        for a in PASS_ORDER:
             if a == 0:
                 round_w1(0, nc.scalar.copy)
                 quantise_w1(0)
             gather_words(a)
-            for h in range(2):
+            for half in range(2):
                 for i in range(PACK):
-                    first_pass(acc[0, h][i], a, 0, h, i, (1, 2, 0))
+                    first_pass(f_banks[0, half][i], a, 0, half, i)
 
         round_w1(1, nc.vector.tensor_copy)
-        th00 = tanh_of(acc[0, 0], 0)
+        th00 = tanh_of(f_banks[0, 0], 0)
         quantise_w1(1)
-        th01 = tanh_of(acc[0, 1], 0)
-        for h in range(2):
-            acc[1, h] = [bank(h, i) for i in range(PACK)]
+        th01 = tanh_of(f_banks[0, 1], 0)
+        for half in range(2):
+            f_banks[1, half] = [bank(half, i) for i in range(PACK)]
             for i in range(PACK):
-                for a in (1, 2, 0):
-                    first_pass(acc[1, h][i], a, 1, h, i, (1, 2, 0))
+                for a in PASS_ORDER:
+                    first_pass(f_banks[1, half][i], a, 1, half, i)
+
         per_job = []
         with nc.allow_non_contiguous_dma(reason="one value a job, jobs on the partitions"):
             for a, src in enumerate((temp, load, finish)):
-                dst = held([P, 4], F32, "per_job%d" % a, "v_w%d_1" % a)
+                dst = held([P, JOB_TILES], F32, "per_job%d" % a, "v_w%d_1" % a)
                 nc.sync.dma_start(out=dst[:], in_=src.rearrange("(m p) -> p m", p=P))
                 per_job.append(dst)
         temp_t, load_t, finish_t = per_job
-        hb00 = apply_gain(th00, 0, 0)
-        th10 = tanh_of(acc[1, 0], 1)
-        hb01 = apply_gain(th01, 0, 1)
+
+        hb00 = gain_and_weave(th00, 0, 0)
+        th10 = tanh_of(f_banks[1, 0], 1)
+        hp10 = gain_planes(th10, 1, 0)
+        hb01 = gain_and_weave(th01, 0, 1)
         quantise_h(hb00, 0, 0)
-        th11 = tanh_of(acc[1, 1], 1)
+        th11 = tanh_of(f_banks[1, 1], 1)
+        hp11 = gain_planes(th11, 1, 1)
 
         v2_w = [held([P, S2], U32, "v2_w%d" % a) for a in range(2)]
-
-        def gather_jobs(a):
+        for a in range(2):
             nc.vector.tensor_copy(out=v2_w[a][:], in_=tab2_w[a][:].indirect(offs2_t[:]))
 
-        gather_jobs(0)
-        hb10 = apply_gain(th10, 1, 0)
-        gather_jobs(1)
+        hb10 = grouped(0)
+        weave(nc.vector.tensor_copy, hb10, hp10, 0, NB)
         quantise_h(hb10, 1, 0)
-        quantise_h(hb01, 0, 1)
-        hb11 = apply_gain_scalar(th11, 1)
+        quantise_h(hb01, 0, 1, "grouped0")
+        hb11 = grouped(1)
+        weave(nc.scalar.copy, hb11, hp11, 0, SPLIT)
 
-        def second_pass(dst, a, h, m):
+        def second_pass(dst, b, half, m):
             cols = slice(P * m, P * (m + 1))
-            nc.tensor.matmul_mx(out=dst[:], lhsT=v2_w[a][:, cols].bitcast(FP8X4), lhsT_scale=v2_s[8:P, a, cols],
-                                rhs=h_c[a][h][:].bitcast(FP8X4), rhs_scale=h_s[a][h][:], start=(a == 0), stop=(a == 1))
+            nc.tensor.matmul_mx(out=dst[:], lhsT=v2_w[b][:, cols].bitcast(FP8X4), lhsT_scale=v2_s[PLANE_V2:P, b, cols],
+                                rhs=h_c[b, half][:].bitcast(FP8X4), rhs_scale=h_s[b, half][:],
+                                start=(b == 0), stop=(b == 1))
 
-        neg_temp = held([P, 4], F32, "neg_temp")
+        neg_temp = held([P, JOB_TILES], F32, "neg_temp")
         nc.vector.tensor_scalar(out=neg_temp[:], in0=temp_t[:], scalar1=-1.0, scalar2=None, op0=ALU.mult)
-        e = [held([P, S], F32, "e%d" % m) for m in range(4)]
-        top_half = held([P, 4], F32, "top_half")
-        top = held([P, 4], F32, "top")
-        look_bias = held([P, 4], F32, "look_bias")
+        last = JOB_TILES - 1
+        e = [held([P, S], F32, "e%d" % m) for m in range(last)]
+        top_half = held([P, JOB_TILES], F32, "top_half")
+        top = held([P, JOB_TILES], F32, "top")
+        look_bias = held([P, JOB_TILES], F32, "look_bias")
 
-        sc = {}
-        for h in range(2):
-            sc[h] = [bank(h, m) for m in range(4)]
-        for m in range(4):
-            for a in range(2):
-                second_pass(sc[0][m], a, 0, m)
-        for m in range(4):
-            second_pass(sc[1][m], 0, 1, m)
+        e_banks = [[bank(half, m) for m in range(JOB_TILES)] for half in range(2)]
+        for b, half in ((0, 0), (1, 0), (0, 1)):
+            for m in range(JOB_TILES):
+                second_pass(e_banks[half][m], b, half, m)
 
-        def scores_out(h, m):
-            nc.vector.tensor_scalar(out=e[m][:, NB * h:NB * (h + 1)], in0=sc[h][m][:], scalar1=1.0,
-                                    scalar2=(None if h == 0 else top_half[:, m:m + 1]), op0=ALU.mult, op1=ALU.max,
-                                    accum_out=(top_half if h == 0 else top)[:, m:m + 1])
+        def scores_out(half, m):
+            nc.vector.tensor_scalar(out=e[m][:, NB * half:NB * (half + 1)], in0=e_banks[half][m][:], scalar1=1.0,
+                                    scalar2=(None if half == 0 else top_half[:, m:m + 1]), op0=ALU.mult, op1=ALU.max,
+                                    accum_out=(top_half if half == 0 else top)[:, m:m + 1])
 
-        for m in range(3):
+        scores_out(0, 0)
+        weave(nc.vector.tensor_copy, hb11, hp11, SPLIT, NB)
+        for m in range(1, last):
             scores_out(0, m)
         quantise_h(hb11, 1, 1)
-        for m in range(4):
-            second_pass(sc[1][m], 1, 1, m)
-        scores_out(0, 3)
+        for m in range(JOB_TILES):
+            second_pass(e_banks[1][m], 1, 1, m)
+        e.append(held([P, S], F32, "e%d" % last, "grouped1"))
+        scores_out(0, last)
 
         def look(m):
             nc.scalar.activation(out=look_bias[:, m:m + 1], in_=top[:, m:m + 1], func=ACT.Copy,
@@ -271,27 +284,27 @@ def tile_list_fastener_job_looks_kernel(tc, tab_words, tab_scales, offs, w1, w4_
             a_t = ring.tile([P, NP], F32, name="a_t", tag="a_t")
             nc.scalar.activation(out=a_t[:], in_=e[m][:].indirect(pos1_t[:]), func=ACT.Exp,
                                  bias=look_bias[:, m:m + 1], scale=temp_t[:, m:m + 1])
-            la = ring.tile([P, NP], F32, name="la", tag="la", bufs=4)
+            la = ring.tile([P, NP], F32, name="la", tag="la", bufs=JOB_TILES)
             nc.scalar.activation(out=la[:], in_=a_t[:], func=ACT.Copy, scale=load_t[:, m:m + 1])
             return la
 
         def pick(m):
-            c_t = ring.tile([P, NP], F32, name="c_t", tag="c_t", bufs=4)
+            c_t = ring.tile([P, NP], F32, name="c_t", tag="c_t", bufs=JOB_TILES)
             nc.vector.tensor_copy(out=c_t[:], in_=e[m][:].indirect(pos2_t[:]))
             return c_t
 
         def finish_rows(m, c_t, la):
-            o_t = ring.tile([P, NP], F32, name="o_t", tag="o_t", bufs=4)
+            o_t = ring.tile([P, NP], F32, name="o_t", tag="o_t", bufs=JOB_TILES)
             nc.vector.scalar_tensor_tensor(out=o_t[:], in0=c_t[:], scalar=finish_t[:, m:m + 1], in1=la[:],
                                            op0=ALU.mult, op1=ALU.add)
             nc.sync.dma_start(out=out[P * m:P * (m + 1), :], in_=o_t[:])
 
-        la, c_t = {}, {}
-        for step in range(6):
-            if step < 4:
+        looked, picked = {}, {}
+        for step in range(JOB_TILES + 2):
+            if step < JOB_TILES:
                 scores_out(1, step)
-                la[step] = look(step)
-            if 1 <= step < 5:
-                c_t[step - 1] = pick(step - 1)
-            if 2 <= step:
-                finish_rows(step - 2, c_t[step - 2], la[step - 2])
+                looked[step] = look(step)
+            if 1 <= step <= JOB_TILES:
+                picked[step - 1] = pick(step - 1)
+            if step >= 2:
+                finish_rows(step - 2, picked[step - 2], looked[step - 2])

from contextlib import ExitStack

import concourse.mybir as mybir

T, S, K, H, T3, S2, NP = 4096, 1024, 1536, 1024, 2048, 512, 512
FLOPS = 2 * K * H * S + 2 * H * S2 * S

F32 = mybir.dt.float32
BF16 = mybir.dt.bfloat16
I32 = mybir.dt.int32
U32 = mybir.dt.uint32
U16 = mybir.dt.uint16
U8 = mybir.dt.uint8
FP8X4 = mybir.dt.float8_e4m3fn_x4
FP4X4 = mybir.dt.float4_e2m1fn_x4
ALU = mybir.AluOpType
ACT = mybir.ActivationFunctionType

P = 128
PACK = 4
NB = 512
JOB_TILES = S2 // P
KIB = 1024
PASS_ORDER = (1, 2, 0)
WALK = 4
SPLIT = 384
TAB_ROWS_12, TAB_ROWS_0, TAB2_ROWS = 0, 112, 64
PLANE_V0, PLANE_V2 = 4, 8


def tile_list_fastener_job_looks_kernel(tc, tab_words, tab_scales, offs, w1, w4_words, w4_scales, b1, gain,
                                                  tab2_words, tab2_scales, offs2, pos1, pos2, temp, load, finish, out):
    nc = tc.nc
    with ExitStack() as ctx:
        lists = ctx.enter_context(tc.tile_pool(name="lists", bufs=1))
        keep = ctx.enter_context(tc.tile_pool(name="keep", bufs=1))
        stage = ctx.enter_context(tc.tile_pool(name="stage", bufs=1))
        ring = ctx.enter_context(tc.tile_pool(name="ring", bufs=2))
        psum = ctx.enter_context(tc.psum_pool(name="psum", bufs=1))

        def held(shape, dtype, name, after=None):
            return keep.tile(shape, dtype, name=name, tag=(after or name), align_bytes=64)

        def staged(shape, dtype, name, offset):
            return stage.tile(shape, dtype, name=name, align_bytes=64, offset=offset)

        offs_t = lists.tile([P, S // 16], U16, name="offs_t")
        offs2_t = lists.tile([P, S2 // 16], U16, name="offs2_t")
        pos1_t = lists.tile([P, NP // 16], U16, name="pos1_t")
        pos2_t = lists.tile([P, NP // 16], U16, name="pos2_t")

        w4_s_raw = held([P, 2, H], U8, "w4_s_raw")
        nc.vector.memset(w4_s_raw[:].rearrange("p a c -> p (a c)").bitcast(I32), 0)
        tab_s = staged([P, T], U8, "tab_s", 7 * KIB)
        tab2_s = staged([P, T3], U8, "tab2_s", 33 * KIB)
        w4_raw = staged([P, 2, 2 * H], U8, "w4_raw", 49 * KIB)
        v_s12 = held([P, 2, S], U8, "v_s12")
        v_s0 = held([P, 1, S], U8, "v_s0")
        v2_s = held([P, 2, S2], U8, "v2_s")
        nc.vector.memset(tab_s[32:64, :].bitcast(I32), 0)
        nc.vector.memset(tab_s[64:TAB_ROWS_0, :].bitcast(I32), 0)
        nc.gpsimd.memset(tab2_s[0:TAB2_ROWS, :].bitcast(I32), 0)
        nc.gpsimd.memset(tab2_s[96:P, :].bitcast(I32), 0)
        for planes in (v_s12, v_s0, v2_s):
            nc.vector.memset(planes[:].rearrange("p a c -> p (a c)").bitcast(I32), 0)

        def load_w1(b, raw):
            nc.sync.dma_start(out=raw[:], in_=w1[:, NB * b:NB * (b + 1)].rearrange("(p j) c -> p j c", j=PACK))
            return raw

        def load_words(src, dst):
            nc.sync.dma_start(out=dst[:].bitcast(I32), in_=src.rearrange("p t i -> p (t i)").bitcast(I32))
            return dst

        def load_scale_rows(dst, row0, src):
            rows = src.shape[0] * src.shape[1]
            nc.sync.dma_start(out=dst[row0:row0 + rows, :].bitcast(I32),
                              in_=src.rearrange("a g c -> g a c").bitcast(I32))

        def spread_scale_rows(planes, first, gathered, row0):
            passes = planes.shape[1]
            for q in range(4):
                nc.sync.dma_start(out=planes[32 * q + first:32 * q + first + 4, :, :].bitcast(I32),
                                  in_=gathered[row0 + 4 * passes * q:row0 + 4 * passes * (q + 1), :].bitcast(I32))

        tab_w = [None, None, None]
        nc.sync.dma_start(offs_t[:], offs)
        load_scale_rows(tab_s, TAB_ROWS_12, tab_scales[1:3])
        load_scale_rows(tab_s, TAB_ROWS_0, tab_scales[0:1])
        nc.sync.dma_start(offs2_t[:], offs2)
        load_scale_rows(tab2_s, TAB2_ROWS, tab2_scales)
        nc.sync.dma_start(out=w4_raw[:].bitcast(I32), in_=w4_words.rearrange("a p n -> p a n").bitcast(I32))
        tab_w[1] = load_words(tab_words[1], held([P, T], U32, "tab_w1"))
        nc.sync.dma_start(pos1_t[:], pos1)
        nc.sync.dma_start(pos2_t[:], pos2)
        for q in range(4):
            nc.sync.dma_start(out=w4_s_raw[32 * q:32 * q + 4, :, :].bitcast(I32),
                              in_=w4_scales[:, 4 * q:4 * q + 4, :].rearrange("a r c -> r a c").bitcast(I32))
        tab_w[2] = load_words(tab_words[2], held([P, T], U32, "tab_w2"))

        v_s_picked = held([P, S], U8, "v_s_picked")
        nc.vector.tensor_copy(out=v_s_picked[:], in_=tab_s[:].indirect(offs_t[:]))
        spread_scale_rows(v_s12, 0, v_s_picked, TAB_ROWS_12)
        w1_raw = [load_w1(0, staged([P, PACK, NB], F32, "w1_raw0", 0)), None]
        tab_w[0] = load_words(tab_words[0], staged([P, T], U32, "tab_w0", 10 * KIB))
        spread_scale_rows(v_s0, PLANE_V0, v_s_picked, TAB_ROWS_0)
        per_row = staged([P, 2, 2, PACK], F32, "per_row", 9 * KIB)
        b1_t, gain_t = per_row[:, 0, :, :], per_row[:, 1, :, :]
        nc.sync.dma_start(out=b1_t, in_=b1.rearrange("(b p i) -> p b i", b=2, i=PACK))
        nc.sync.dma_start(out=gain_t, in_=gain.rearrange("(b p i) -> p b i", b=2, i=PACK))

        w4_c = held([P, 2, 2 * H], U8, "w4_c")
        nc.vector.tensor_copy(
            out=w4_c[:].bitcast(U16).rearrange("p a (b i m) -> p (a b) i m", b=2, i=PACK),
            in_=w4_raw[:].bitcast(U16).rearrange("p a (b m i) -> p (a b) i m", b=2, i=PACK))
        w1_raw[1] = load_w1(1, staged([P, PACK, NB], F32, "w1_raw1", 42 * KIB))

        v2_s_picked = staged([P, S2], U8, "v2_s_picked", 53 * KIB - S2)
        nc.vector.tensor_copy(out=v2_s_picked[:], in_=tab2_s[:].indirect(offs2_t[:]))
        tab2_w = [load_words(tab2_words[a], staged([P, T3], U32, "tab2_w%d" % a, (26 + 8 * a) * KIB)) for a in range(2)]
        spread_scale_rows(v2_s, PLANE_V2, v2_s_picked, TAB2_ROWS)

        w4_s = held([P, 2, H], U8, "w4_s")
        nc.vector.tensor_copy(
            out=w4_s[:].rearrange("p a (b i m) -> p (a b) i m", b=2, i=PACK),
            in_=w4_s_raw[:].rearrange("p a (b m i) -> p (a b) i m", b=2, i=PACK))

        def grouped(slot):
            return keep.tile([P, NB * PACK], BF16, name="grouped%d" % slot, tag="grouped%d" % slot, align_bytes=64)

        w1_g = [grouped(1), grouped(0)]
        w1_c = [held([P, NB], U32, "w1_c%d" % b) for b in range(2)]
        w1_s = [held([P, NB], U8, "w1_s%d" % b) for b in range(2)]

        def round_w1(b, copy):
            copy(out=w1_g[b][:].rearrange("p (i m j) -> p m i j", i=PACK, j=PACK),
                 in_=w1_raw[b][:].rearrange("p j (m i) -> p m i j", i=PACK))

        def quantise_w1(b):
            nc.vector.quantize_mx(out=w1_c[b][:].bitcast(FP8X4), scales=w1_s[b][:], in_=w1_g[b][:])

        v_w = [[held([P, NB], U32, "v_w%d_%d" % (a, half)) for half in range(2)] for a in range(3)]

        def gather_words(a):
            for half in range(2):
                nc.vector.tensor_copy(out=v_w[a][half][:],
                                      in_=tab_w[a][:].indirect(offs_t[:, 32 * half:32 * (half + 1)]))

        def bank(half, n):
            return psum.tile([P, NB], F32, name="bank%d_%d" % (half, n), tag="bank%d_%d" % (half, n))

        def first_pass(dst, a, b, half, i):
            cols = slice(NB * half, NB * (half + 1))
            if a == 0:
                lhsT = w1_c[b][:, P * i:P * (i + 1)].bitcast(FP8X4)
                lhsT_scale = w1_s[b][:, P * i:P * (i + 1)]
                rhs_scale = v_s0[PLANE_V0:P, 0, cols]
            else:
                c0 = NB * b + P * i
                lhsT = w4_c[:, a - 1, 2 * c0:2 * (c0 + P)].bitcast(FP4X4)
                lhsT_scale = w4_s[:, a - 1, c0:c0 + P]
                rhs_scale = v_s12[:, a - 1, cols]
            nc.tensor.matmul_mx(out=dst[:], lhsT=lhsT, lhsT_scale=lhsT_scale, rhs=v_w[a][half][:].bitcast(FP8X4),
                                rhs_scale=rhs_scale, start=(a == PASS_ORDER[0]), stop=(a == PASS_ORDER[2]))

        def tanh_of(banks, b):
            th = ring.tile([P, PACK, NB], F32, name="th", tag="th", bufs=3)
            for i in range(PACK):
                nc.scalar.activation(out=th[:, i, :], in_=banks[i][:], func=ACT.Tanh, bias=b1_t[:, b, i:i + 1])
            return th

        h_c, h_s = {}, {}

        def gain_and_weave(th, b, half):
            hb = grouped(half)
            nc.vector.tensor_tensor(
                out=hb[:].rearrange("p (c u i) -> p c i u", u=WALK, i=PACK),
                in0=th[:].rearrange("p i (c u) -> p c i u", u=WALK),
                in1=gain_t[:, b, :].unsqueeze(1).unsqueeze(3).to_broadcast([P, NB // WALK, PACK, WALK]),
                op=ALU.mult)
            return hb

        def gain_planes(th, b, half):
            hp = held([P, PACK, NB], BF16, "hp%d" % half)
            for i in range(PACK):
                nc.scalar.activation(out=hp[:, i, :], in_=th[:, i, :], func=ACT.Copy, scale=gain_t[:, b, i:i + 1])
            return hp

        def weave(copy, hb, hp, c0, c1):
            copy(out=hb[:, PACK * c0:PACK * c1].rearrange("p (c u i) -> p c i u", u=WALK, i=PACK),
                 in_=hp[:, :, c0:c1].rearrange("p i (c u) -> p c i u", u=WALK))

        def quantise_h(hb, b, half, after=None):
            h_c[b, half] = held([P, NB], U32, "h_c%d_%d" % (b, half), after)
            h_s[b, half] = held([P, NB], U8, "h_s%d_%d" % (b, half))
            nc.vector.quantize_mx(out=h_c[b, half][:].bitcast(FP8X4), scales=h_s[b, half][:], in_=hb[:])

        f_banks = {}
        for half in range(2):
            f_banks[0, half] = [bank(half, i) for i in range(PACK)]
        for a in PASS_ORDER:
            if a == 0:
                round_w1(0, nc.scalar.copy)
                quantise_w1(0)
            gather_words(a)
            for half in range(2):
                for i in range(PACK):
                    first_pass(f_banks[0, half][i], a, 0, half, i)

        round_w1(1, nc.vector.tensor_copy)
        th00 = tanh_of(f_banks[0, 0], 0)
        quantise_w1(1)
        th01 = tanh_of(f_banks[0, 1], 0)
        for half in range(2):
            f_banks[1, half] = [bank(half, i) for i in range(PACK)]
            for i in range(PACK):
                for a in PASS_ORDER:
                    first_pass(f_banks[1, half][i], a, 1, half, i)

        per_job = []
        with nc.allow_non_contiguous_dma(reason="one value a job, jobs on the partitions"):
            for a, src in enumerate((temp, load, finish)):
                dst = held([P, JOB_TILES], F32, "per_job%d" % a, "v_w%d_1" % a)
                nc.sync.dma_start(out=dst[:], in_=src.rearrange("(m p) -> p m", p=P))
                per_job.append(dst)
        temp_t, load_t, finish_t = per_job

        hb00 = gain_and_weave(th00, 0, 0)
        th10 = tanh_of(f_banks[1, 0], 1)
        hp10 = gain_planes(th10, 1, 0)
        hb01 = gain_and_weave(th01, 0, 1)
        quantise_h(hb00, 0, 0)
        th11 = tanh_of(f_banks[1, 1], 1)
        hp11 = gain_planes(th11, 1, 1)

        v2_w = [held([P, S2], U32, "v2_w%d" % a) for a in range(2)]
        for a in range(2):
            nc.vector.tensor_copy(out=v2_w[a][:], in_=tab2_w[a][:].indirect(offs2_t[:]))

        hb10 = grouped(0)
        weave(nc.vector.tensor_copy, hb10, hp10, 0, NB)
        quantise_h(hb10, 1, 0)
        quantise_h(hb01, 0, 1, "grouped0")
        hb11 = grouped(1)
        weave(nc.scalar.copy, hb11, hp11, 0, SPLIT)

        def second_pass(dst, b, half, m):
            cols = slice(P * m, P * (m + 1))
            nc.tensor.matmul_mx(out=dst[:], lhsT=v2_w[b][:, cols].bitcast(FP8X4), lhsT_scale=v2_s[PLANE_V2:P, b, cols],
                                rhs=h_c[b, half][:].bitcast(FP8X4), rhs_scale=h_s[b, half][:],
                                start=(b == 0), stop=(b == 1))

        neg_temp = held([P, JOB_TILES], F32, "neg_temp")
        nc.vector.tensor_scalar(out=neg_temp[:], in0=temp_t[:], scalar1=-1.0, scalar2=None, op0=ALU.mult)
        last = JOB_TILES - 1
        e = [held([P, S], F32, "e%d" % m) for m in range(last)]
        top_half = held([P, JOB_TILES], F32, "top_half")
        top = held([P, JOB_TILES], F32, "top")
        look_bias = held([P, JOB_TILES], F32, "look_bias")

        e_banks = [[bank(half, m) for m in range(JOB_TILES)] for half in range(2)]
        for b, half in ((0, 0), (1, 0), (0, 1)):
            for m in range(JOB_TILES):
                second_pass(e_banks[half][m], b, half, m)

        def scores_out(half, m):
            nc.vector.tensor_scalar(out=e[m][:, NB * half:NB * (half + 1)], in0=e_banks[half][m][:], scalar1=1.0,
                                    scalar2=(None if half == 0 else top_half[:, m:m + 1]), op0=ALU.mult, op1=ALU.max,
                                    accum_out=(top_half if half == 0 else top)[:, m:m + 1])

        scores_out(0, 0)
        weave(nc.vector.tensor_copy, hb11, hp11, SPLIT, NB)
        for m in range(1, last):
            scores_out(0, m)
        quantise_h(hb11, 1, 1)
        for m in range(JOB_TILES):
            second_pass(e_banks[1][m], 1, 1, m)
        e.append(held([P, S], F32, "e%d" % last, "grouped1"))
        scores_out(0, last)

        def look(m):
            nc.scalar.activation(out=look_bias[:, m:m + 1], in_=top[:, m:m + 1], func=ACT.Copy,
                                 scale=neg_temp[:, m:m + 1])
            a_t = ring.tile([P, NP], F32, name="a_t", tag="a_t")
            nc.scalar.activation(out=a_t[:], in_=e[m][:].indirect(pos1_t[:]), func=ACT.Exp,
                                 bias=look_bias[:, m:m + 1], scale=temp_t[:, m:m + 1])
            la = ring.tile([P, NP], F32, name="la", tag="la", bufs=JOB_TILES)
            nc.scalar.activation(out=la[:], in_=a_t[:], func=ACT.Copy, scale=load_t[:, m:m + 1])
            return la

        def pick(m):
            c_t = ring.tile([P, NP], F32, name="c_t", tag="c_t", bufs=JOB_TILES)
            nc.vector.tensor_copy(out=c_t[:], in_=e[m][:].indirect(pos2_t[:]))
            return c_t

        def finish_rows(m, c_t, la):
            o_t = ring.tile([P, NP], F32, name="o_t", tag="o_t", bufs=JOB_TILES)
            nc.vector.scalar_tensor_tensor(out=o_t[:], in0=c_t[:], scalar=finish_t[:, m:m + 1], in1=la[:],
                                           op0=ALU.mult, op1=ALU.add)
            nc.sync.dma_start(out=out[P * m:P * (m + 1), :], in_=o_t[:])

        looked, picked = {}, {}
        for step in range(JOB_TILES + 2):
            if step < JOB_TILES:
                scores_out(1, step)
                looked[step] = look(step)
            if 1 <= step <= JOB_TILES:
                picked[step - 1] = pick(step - 1)
            if step >= 2:
                finish_rows(step - 2, picked[step - 2], looked[step - 2])
